import numpy as np
import ml_dtypes


def mxq(x, axis, fmt="e4m3"):
    dtype, down = {"e4m3": (ml_dtypes.float8_e4m3fn, 7), "e5m2": (ml_dtypes.float8_e5m2, 14)}[fmt]
    v = np.moveaxis(np.asarray(x, np.float32).astype(ml_dtypes.bfloat16).astype(np.float64), axis, -1)
    blocks = v.reshape(v.shape[:-1] + (-1, 32))
    amax = np.abs(blocks).max(-1, keepdims=True)
    byte = np.maximum(np.where(amax > 0, np.frexp(amax)[1] - 1 + 127, 0) - down, 1)
    scale = np.exp2(byte - 127.0)
    codes = (blocks / scale).astype(np.float32).astype(dtype).astype(np.float64)
    return np.moveaxis((codes * scale).reshape(v.shape), -1, axis)


WIDE = False


def mx_kscale(k):
    if not WIDE:
        return np.ones(k)
    levels = np.array([10, -10, 5, -5, 0])
    if k % 512:
        return np.exp2(np.random.permutation(np.resize(levels, k // 32))).repeat(32)
    a = np.empty((k // 512, 16))
    for p in range(k // 512):
        a[p, :8] = np.random.permutation(np.resize(levels, 8))
        for g in range(8):
            far = levels[np.abs(levels - a[p, g]) >= 10]
            a[p, g + 8] = far[np.random.randint(len(far))]
    return np.exp2(a.ravel()).repeat(32)


def f64(x):
    return np.asarray(x).astype(np.float64)


def striped(idx):
    return np.tile(idx.reshape(-1, 16).T, (8, 1)).astype(np.uint16)


def unstriped(offs):
    return offs[:16].T.reshape(-1).astype(np.int64)


E2M1 = np.array([0.0, 0.5, 1.0, 1.5, 2.0, 3.0, 4.0, 6.0, -0.0, -0.5, -1.0, -1.5, -2.0, -3.0, -4.0, -6.0])


def pack_weight(w, fmt):
    k, n = w.shape
    w = f64(np.asarray(w, np.float32).astype(ml_dtypes.bfloat16)).reshape(k // 32, 32, n)
    amax = np.abs(w).max(1)
    if fmt == "e4m3":
        byte = np.frexp(amax)[1] - 1 + 127 - 7
    else:
        mant, ex = np.frexp(amax / 6.0)
        byte = np.where(mant > 0.5, ex, ex - 1) + 127
    byte = np.clip(np.where(amax > 0, byte, 1), 1, 254)
    scaled = (w * np.exp2(127.0 - byte)[:, None, :]).reshape(k, n).astype(np.float32)
    by_word = np.ascontiguousarray(scaled.reshape(k // 512, 128, 4, n).transpose(0, 1, 3, 2))
    if fmt == "e4m3":
        words = by_word.astype(ml_dtypes.float8_e4m3fn).view(np.uint8)
    else:
        c = by_word.astype(ml_dtypes.float4_e2m1fn).view(np.uint8) & 0xF
        words = (c[..., 0::2] | (c[..., 1::2] << 4)).reshape(k // 512, 128, 2 * n)
    return np.ascontiguousarray(words), np.ascontiguousarray(byte.astype(np.uint8).reshape(k // 512, 16, n))


def unpack_weight(words, scales, fmt):
    g, _, n = scales.shape
    words = np.ascontiguousarray(words).reshape(g, 128, n, -1)
    if fmt == "e4m3":
        vals = words.view(ml_dtypes.float8_e4m3fn).astype(np.float64)
    else:
        nib = np.empty((g, 128, n, 4), np.uint8)
        nib[..., 0::2] = words & 0xF
        nib[..., 1::2] = words >> 4
        vals = E2M1[nib]
    vals = vals * np.repeat(np.exp2(scales.astype(np.float64) - 127.0), 8, axis=1)[..., None]
    return vals.transpose(0, 1, 3, 2).reshape(g * 512, n)


def gelu(v):
    return 0.5 * v * (1.0 + np.tanh(np.sqrt(2.0 / np.pi) * (v + 0.044715 * v**3)))


def often(T, S):
    return np.random.permutation(T)[(T * np.random.uniform(0, 1, S) ** 4).astype(np.int64)]


K, K2, H, T, S = 1024, 512, 1024, 4096, 1024

def setup_inputs():
    n = np.random.standard_normal
    s = mx_kscale(K)[:, None]
    s2 = mx_kscale(K2)[:, None]
    u = mx_kscale(H)[:, None]
    tab_words, tab_scales = pack_weight(n((K, T)) * s, "e4m3")
    tab2_words, tab2_scales = pack_weight(n((K2, T)) * s2, "e2m1")
    w1_words, w1_scales = pack_weight(0.8 * n((K, H)) / np.sqrt(K) / s, "e2m1")
    w2 = (0.8 * n((K2, H)) / np.sqrt(K2) / s2).astype(np.float32)
    gain = (np.exp(0.3 * n(H)) * u[:, 0]).astype(np.float32)
    w3_words, w3_scales = pack_weight(n((H, H)) / np.sqrt(H) / u, "e4m3")
    return {"tab_words": tab_words, "tab_scales": tab_scales,
            "tab2_words": tab2_words, "tab2_scales": tab2_scales,
            "offs": striped(often(T, S)), "offs2": striped(often(T, S)),
            "w1_words": w1_words, "w1_scales": w1_scales,
            "w2": w2, "gain": gain,
            "w3_words": w3_words, "w3_scales": w3_scales}

def reference(tab_words, tab_scales, tab2_words, tab2_scales, offs, offs2,
              w1_words, w1_scales, w2, gain, w3_words, w3_scales):
    v = unpack_weight(tab_words, tab_scales, "e4m3")[:, unstriped(offs)]
    v2 = unpack_weight(tab2_words, tab2_scales, "e2m1")[:, unstriped(offs2)]
    w1 = unpack_weight(w1_words, w1_scales, "e2m1")
    w3 = unpack_weight(w3_words, w3_scales, "e4m3")
    a = w1.T @ v
    b = mxq(f64(w2), 0, "e4m3").T @ v2
    h = np.tanh(a - b) * f64(gain)[:, None]
    cost = w3.T @ mxq(h, 0, "e4m3")
    return cost + a

@@ -1,0 +1,328 @@
+from contextlib import ExitStack
+
+import concourse.mybir as mybir
+
+K, K2, H, T, S = 1024, 512, 1024, 4096, 1024
+FLOPS = 2 * S * H * (K + K2 + H)
+
+F32 = mybir.dt.float32
+BF16 = mybir.dt.bfloat16
+I32 = mybir.dt.int32
+U32 = mybir.dt.uint32
+U16 = mybir.dt.uint16
+U8 = mybir.dt.uint8
+FP8X4 = mybir.dt.float8_e4m3fn_x4
+FP4X4 = mybir.dt.float4_e2m1fn_x4
+ALU = mybir.AluOpType
+ACT = mybir.ActivationFunctionType
+
+P = 128
+PACK = 4
+BLOCK = P * PACK
+HALF = 512
+CHUNK = 128
+QUAD = 32
+ROWS = 4
+
+
+def tile_list_merge_negotiation_costs_kernel(
+    tc, tab_words, tab_scales, tab2_words, tab2_scales, offs, offs2,
+    w1_words, w1_scales, w2, gain, w3_words, w3_scales, out,
+):
+    nc = tc.nc
+    with ExitStack() as ctx:
+        lists = ctx.enter_context(tc.tile_pool(name="lists", bufs=1))
+        keep = ctx.enter_context(tc.tile_pool(name="keep", bufs=1))
+        work = ctx.enter_context(tc.tile_pool(name="work", bufs=2))
+        psum = ctx.enter_context(tc.psum_pool(name="psum", bufs=8))
+
+        def held(shape, dtype, name, tag=None):
+            return keep.tile(shape, dtype, name=name, tag=tag or name, align_bytes=64)
+
+        def bank(name):
+            return psum.tile([P, HALF], F32, name=name, tag="bank")
+
+        idx = lists.tile([P, S // 16], U16, name="idx")
+        idx2 = lists.tile([P, S // 16], U16, name="idx2")
+        nc.sync.dma_start(idx[:], offs)
+        nc.sync.dma_start(idx2[:], offs2)
+
+        def half_of(index_tile, h):
+            return index_tile[:, h * (HALF // 16) : (h + 1) * (HALF // 16)]
+
+        tab_s = held([P, T // 4], I32, "tab_s", "slot_a")
+        w_s = held([P, 2, H // 4], I32, "w_s")
+        tab2_s = held([P, T // 4], I32, "tab2_s")
+        v_s1 = held([P, S // 4], I32, "v_s1")
+        zero = held([P, 1], F32, "zero")
+        no_bias = held([P, 1], F32, "no_bias")
+        nc.vector.memset(tab_s[:], 0)
+        nc.vector.memset(w_s[:], 0)
+        nc.vector.memset(tab2_s[:], 0)
+        nc.vector.memset(v_s1[:], 0)
+        nc.vector.memset(zero[:], 0.0)
+        nc.scalar.activation(no_bias[:], zero[:], ACT.Tanh)
+
+        for q in range(4):
+            nc.scalar.dma_start(
+                tab_s[QUAD * q : QUAD * q + 2 * ROWS, :],
+                tab_scales[:, ROWS * q : ROWS * (q + 1), :].bitcast(I32),
+            )
+        w1_raw = held([P, 2, H // 2], I32, "w1_raw", "slot_c")
+        nc.sync.dma_start(w1_raw[:], w1_words.rearrange("a p c -> p a c").bitcast(I32))
+        tab_w0 = held([P, T], I32, "tab_w0", "slot_b")
+        nc.sync.dma_start(tab_w0[:], tab_words[0].rearrange("p t i -> p (t i)").bitcast(I32))
+        for q in range(4):
+            nc.gpsimd.dma_start(
+                w_s[QUAD * q : QUAD * q + ROWS, :, :],
+                w1_scales[:, ROWS * q : ROWS * (q + 1), :].rearrange("a r c -> r a c").bitcast(I32),
+            )
+        for q in range(4):
+            nc.gpsimd.dma_start(
+                w_s[QUAD * q + ROWS : QUAD * q + 2 * ROWS, :, :],
+                w3_scales[:, ROWS * q : ROWS * (q + 1), :].rearrange("a r c -> r a c").bitcast(I32),
+            )
+        for q in range(4):
+            nc.scalar.dma_start(
+                tab2_s[QUAD * q : QUAD * q + ROWS, :],
+                tab2_scales[0, ROWS * q : ROWS * (q + 1), :].bitcast(I32),
+            )
+        gain_sb = held([P, 2, PACK], F32, "gain_sb")
+        nc.gpsimd.dma_start(gain_sb[:], gain.rearrange("(g p t) -> p g t", g=2, t=PACK))
+
+        v_s = held([P, S], U8, "v_s")
+        nc.vector.tensor_copy(v_s[:], tab_s[:].bitcast(U8).indirect(idx[:]))
+        for q in range(4):
+            nc.scalar.dma_start(
+                v_s1[QUAD * q : QUAD * q + ROWS, :],
+                v_s[QUAD * q + ROWS : QUAD * q + 2 * ROWS, :].bitcast(I32),
+            )
+        v_scale = [v_s[:], v_s1[:].bitcast(U8)]
+
+        tab_w1 = held([P, T], I32, "tab_w1", "slot_a")
+        nc.sync.dma_start(tab_w1[:], tab_words[1].rearrange("p t i -> p (t i)").bitcast(I32))
+
+        w1_p = held([P, 2 * H], U16, "w1_p")
+        nc.vector.tensor_copy(
+            w1_p[:].rearrange("p (g t m) -> p g t m", t=PACK, m=P),
+            w1_raw[:].rearrange("p a c -> p (a c)").bitcast(U16).rearrange("p (g m t) -> p g t m", t=PACK, m=P),
+        )
+        v2_s = held([P, S], U8, "v2_s")
+        nc.vector.tensor_copy(v2_s[:], tab2_s[:].bitcast(U8).indirect(idx2[:]))
+
+        def load_w2(g, tag):
+            raw = held([P, PACK, BLOCK], F32, "w2_raw%d" % g, tag)
+            nc.sync.dma_start(raw[:], w2[:, g * BLOCK : (g + 1) * BLOCK].rearrange("(p j) c -> p j c", j=PACK))
+            return raw
+
+        w2_raw0 = load_w2(0, "slot_c")
+
+        v = {}
+
+        def gather_v(a, h, window):
+            v[a, h] = held([P, HALF], U32, "v%d%d" % (a, h))
+            nc.vector.tensor_copy(v[a, h][:], window[:].bitcast(U32).indirect(half_of(idx, h)))
+
+        gather_v(0, 0, tab_w0)
+        gather_v(0, 1, tab_w0)
+        w_sp = held([P, 2 * H], U8, "w_sp")
+        nc.vector.tensor_copy(
+            w_sp[:].rearrange("p (g t m) -> p g t m", t=PACK, m=P),
+            w_s[:].rearrange("p a c -> p (a c)").bitcast(U8).rearrange("p (g m t) -> p g t m", t=PACK, m=P),
+        )
+        tab2_w = held([P, T // 2], I32, "tab2_w", "slot_b")
+        nc.sync.dma_start(tab2_w[:], tab2_words[0].bitcast(I32))
+        gather_v(1, 0, tab_w1)
+        gather_v(1, 1, tab_w1)
+        w2_raw1 = load_w2(1, "slot_a")
+
+        w2_q, w2_s = {}, {}
+
+        def w2_views(g, raw):
+            grouped = held([P, PACK * BLOCK], BF16, "w2_bf%d" % g)
+            return (
+                grouped,
+                grouped[:].rearrange("p (t m j) -> p m j t", t=PACK, j=PACK),
+                raw[:].rearrange("p j (m t) -> p m j t", t=PACK),
+            )
+
+        def quantize_w2(g, grouped):
+            w2_q[g] = held([P, BLOCK], U32, "w2_q%d" % g)
+            w2_s[g] = held([P, BLOCK], U8, "w2_s%d" % g)
+            nc.vector.quantize_mx(out=w2_q[g][:].bitcast(FP8X4), scales=w2_s[g][:], in_=grouped[:])
+
+        def cols(g, t):
+            return slice(g * BLOCK + t * P, g * BLOCK + (t + 1) * P)
+
+        def pass_a(acc, a, g, t, h, js, start, stop):
+            c = slice(a * H + cols(g, t).start, a * H + cols(g, t).stop)
+            sj = slice(h * HALF + js.start, h * HALF + js.stop)
+            nc.tensor.matmul_mx(
+                out=acc, lhsT=w1_p[:, c].bitcast(FP4X4), lhsT_scale=w_sp[:, c],
+                rhs=v[a, h][:, js].bitcast(FP8X4), rhs_scale=v_scale[a][:, sj], start=start, stop=stop,
+            )
+
+        v2 = {}
+
+        def gather_v2(h):
+            v2[h] = held([P, HALF], U16, "v2%d" % h)
+            nc.vector.tensor_copy(v2[h][:], tab2_w[:].bitcast(U16).indirect(half_of(idx2, h)))
+
+        def pass_b(acc, g, t, h, js, start, stop):
+            c = cols(0, t)
+            sj = slice(h * HALF + js.start, h * HALF + js.stop)
+            nc.tensor.matmul_mx(
+                out=acc, lhsT=w2_q[g][:, c].bitcast(FP8X4), lhsT_scale=w2_s[g][:, c],
+                rhs=v2[h][:, js].bitcast(FP4X4), rhs_scale=v2_s[:, sj], start=start, stop=stop,
+            )
+
+        whole = slice(0, HALF)
+        a_sb = {}
+
+        def make_a(g, h):
+            for t in range(PACK):
+                acc = bank("a_ps")
+                pass_a(acc[:], 0, g, t, h, whole, True, False)
+                pass_a(acc[:], 1, g, t, h, whole, False, True)
+                a_sb[g, t, h] = held([P, HALF], F32, "a%d%d%d" % (g, t, h))
+                nc.scalar.copy(a_sb[g, t, h][:], acc[:])
+
+        diff = {}
+
+        def make_diff(g, h):
+            diff[g, h] = work.tile([P, PACK, HALF], F32, name="diff", tag="diff")
+            for t in range(PACK):
+                acc = bank("b_ps")
+                pass_b(acc[:], g, t, h, whole, True, True)
+                nc.vector.tensor_tensor(diff[g, h][:, t, :], acc[:], a_sb[g, t, h][:], ALU.add)
+
+        bounded = {}
+
+        def make_tanh(g, h):
+            for u in range(2):
+                th = work.tile([P, (HALF // 2) * PACK], F32, name="th", tag="th", bufs=4)
+                bounded[g, h, u] = th
+                js = slice(u * (HALF // 2), (u + 1) * (HALF // 2))
+                nc.scalar.activation(
+                    th[:].rearrange("p (c i t) -> p c t i", i=4, t=PACK),
+                    diff[g, h][:, :, js].rearrange("p t (c i) -> p c t i", i=4),
+                    ACT.Tanh, bias=no_bias[:],
+                )
+
+        h_q, h_s = {}, {}
+
+        def weigh(dst, th, g, n):
+            nc.vector.tensor_tensor(
+                dst.rearrange("p (j t) -> p j t", t=PACK), th.rearrange("p (j t) -> p j t", t=PACK),
+                gain_sb[:, g : g + 1, :].to_broadcast([P, n, PACK]), ALU.mult,
+            )
+
+        h_bf = {}
+
+        def make_h(g, h):
+            h_bf[g, h] = work.tile([P, HALF * PACK], BF16, name="h_bf", tag="h_bf", align_bytes=64)
+            for u in range(2):
+                n = HALF // 2
+                weigh(h_bf[g, h][:, u * n * PACK : (u + 1) * n * PACK], bounded[g, h, u][:], g, n)
+
+        def quantize_h(g, h):
+            h_q[g, h] = held([P, HALF], U32, "h_q%d%d" % (g, h))
+            h_s[g, h] = held([P, HALF], U8, "h_s%d%d" % (g, h))
+            nc.vector.quantize_mx(out=h_q[g, h][:].bitcast(FP8X4), scales=h_s[g, h][:], in_=h_bf[g, h][:])
+
+        def pass_c(acc, g, b, t, h, start, stop):
+            c = slice(g * H + cols(b, t).start, g * H + cols(b, t).stop)
+            nc.tensor.matmul_mx(
+                out=acc, lhsT=w3_p[g][:, cols(b, t)].bitcast(FP8X4), lhsT_scale=w_sp[ROWS:P, c],
+                rhs=h_q[g, h][:].bitcast(FP8X4), rhs_scale=h_s[g, h][:], start=start, stop=stop,
+            )
+
+        def store(b, t, h, res):
+            rows = out[b * BLOCK : (b + 1) * BLOCK, h * HALF : (h + 1) * HALF].rearrange("(p t) j -> p t j", t=PACK)
+            nc.sync.dma_start(rows[:, t, :], res[:])
+
+        def result():
+            return work.tile([P, HALF], F32, name="res", tag="res", bufs=8)
+
+        make_a(0, 0)
+        grouped0, dst0, src0 = w2_views(0, w2_raw0)
+        nc.vector.tensor_scalar(dst0, src0, -1.0, None, ALU.mult)
+        w3_raw = held([P, 2, H], I32, "w3_raw", "slot_c")
+        nc.sync.dma_start(w3_raw[:], w3_words.rearrange("a p c i -> p a (c i)").bitcast(I32))
+        gather_v2(0)
+        quantize_w2(0, grouped0)
+        make_a(0, 1)
+        make_diff(0, 0)
+        gather_v2(1)
+        make_tanh(0, 0)
+        make_a(1, 0)
+        make_diff(0, 1)
+        grouped1, dst1, src1 = w2_views(1, w2_raw1)
+        nc.scalar.activation(dst1, src1, ACT.Copy, scale=-1.0)
+        make_h(0, 0)
+        make_tanh(0, 1)
+        quantize_w2(1, grouped1)
+        quantize_h(0, 0)
+        make_diff(1, 0)
+        make_h(0, 1)
+        make_tanh(1, 0)
+        w3_p = []
+        for g in range(2):
+            w3_p.append(held([P, H], U32, "w3_p%d" % g))
+            nc.vector.tensor_copy(
+                w3_p[g][:].rearrange("p (b t c i) -> p b c t i", t=PACK, i=4, b=2),
+                w3_raw[:, g, :].bitcast(U32).rearrange("p (b c i t) -> p b c t i", t=PACK, i=4, b=2),
+            )
+        quantize_h(0, 1)
+
+        last = []
+        for c in range(HALF // CHUNK):
+            js = slice(c * CHUNK, (c + 1) * CHUNK)
+            acc = bank("d_ps")
+            for t in range(PACK):
+                part = acc[:, t * CHUNK : (t + 1) * CHUNK]
+                pass_a(part, 0, 1, t, 1, js, True, False)
+                pass_a(part, 1, 1, t, 1, js, False, False)
+                pass_b(part, 1, t, 1, js, False, True)
+            th = work.tile([P, CHUNK * PACK], F32, name="th_last", tag="th_last", bufs=4)
+            nc.scalar.activation(
+                th[:].rearrange("p (j t) -> p j t", t=PACK), acc[:].rearrange("p (t j) -> p j t", t=PACK),
+                ACT.Tanh, bias=no_bias[:],
+            )
+            last.append(th)
+        make_h(1, 0)
+        quantize_h(1, 0)
+
+        h_bf[1, 1] = work.tile([P, HALF * PACK], BF16, name="h_bf", tag="h_bf", align_bytes=64)
+        for c in range(HALF // CHUNK):
+            weigh(h_bf[1, 1][:, c * CHUNK * PACK : (c + 1) * CHUNK * PACK], last[c][:], 1, CHUNK)
+        for b in range(2):
+            for t in range(PACK):
+                acc = bank("c_ps")
+                pass_c(acc[:], 0, b, t, 0, True, False)
+                pass_c(acc[:], 1, b, t, 0, False, True)
+                res = result()
+                nc.vector.tensor_tensor(res[:], acc[:], a_sb[b, t, 0][:], ALU.add)
+                store(b, t, 0, res)
+                if (b, t) == (0, 0):
+                    quantize_h(1, 1)
+
+        open_banks = {}
+        for t in range(PACK):
+            acc = bank("c_ps")
+            pass_a(acc[:], 0, 1, t, 1, whole, True, False)
+            pass_a(acc[:], 1, 1, t, 1, whole, False, False)
+            pass_c(acc[:], 0, 1, t, 1, False, False)
+            open_banks[1, t] = acc
+        for t in range(PACK):
+            acc = bank("c_ps")
+            pass_c(acc[:], 0, 0, t, 1, True, False)
+            pass_c(acc[:], 1, 0, t, 1, False, True)
+            res = result()
+            nc.vector.tensor_tensor(res[:], acc[:], a_sb[0, t, 1][:], ALU.add)
+            store(0, t, 1, res)
+            acc = open_banks[1, t]
+            pass_c(acc[:], 1, 1, t, 1, False, True)
+            res = result()
+            nc.scalar.copy(res[:], acc[:])
+            store(1, t, 1, res)

@@ -20,7 +20,9 @@ P = 128
 PACK = 4
 BLOCK = P * PACK
 HALF = 512
+QUARTER = 256
 CHUNK = 128
+ROUTE = "vp"
 QUAD = 32
 ROWS = 4
 
@@ -33,11 +35,15 @@ def tile_list_merge_negotiation_costs_kernel(
     with ExitStack() as ctx:
         lists = ctx.enter_context(tc.tile_pool(name="lists", bufs=1))
         keep = ctx.enter_context(tc.tile_pool(name="keep", bufs=1))
+        shared = ctx.enter_context(tc.tile_pool(name="shared", bufs=1))
         work = ctx.enter_context(tc.tile_pool(name="work", bufs=2))
         psum = ctx.enter_context(tc.psum_pool(name="psum", bufs=8))
 
         def held(shape, dtype, name, tag=None):
             return keep.tile(shape, dtype, name=name, tag=tag or name, align_bytes=64)
+
+        def placed(shape, dtype, name, kib):
+            return shared.tile(shape, dtype, name=name, tag=name, align_bytes=64, offset=kib * 1024)
 
         def bank(name):
             return psum.tile([P, HALF], F32, name=name, tag="bank")
@@ -50,91 +56,85 @@ def tile_list_merge_negotiation_costs_kernel(
         def half_of(index_tile, h):
             return index_tile[:, h * (HALF // 16) : (h + 1) * (HALF // 16)]
 
-        tab_s = held([P, T // 4], I32, "tab_s", "slot_a")
-        w_s = held([P, 2, H // 4], I32, "w_s")
-        tab2_s = held([P, T // 4], I32, "tab2_s")
+        tab_s = placed([P, T // 4], I32, "tab_s", 25)
         v_s1 = held([P, S // 4], I32, "v_s1")
-        zero = held([P, 1], F32, "zero")
+        w_s = placed([P, 2, H // 4], I32, "w_s", 43)
+        tab2_s = held([P, T // 4], I32, "tab2_s")
+        zero = placed([P, 1], F32, "zero", 0)
         no_bias = held([P, 1], F32, "no_bias")
-        nc.vector.memset(tab_s[:], 0)
+        nc.vector.memset(tab_s[:, 0 : T // 8], 0)
+        nc.gpsimd.memset(tab_s[:, T // 8 : T // 4], 0)
+        nc.gpsimd.memset(v_s1[:], 0)
+        nc.vector.memset(zero[:], 0.0)
         nc.vector.memset(w_s[:], 0)
         nc.vector.memset(tab2_s[:], 0)
-        nc.vector.memset(v_s1[:], 0)
-        nc.vector.memset(zero[:], 0.0)
         nc.scalar.activation(no_bias[:], zero[:], ACT.Tanh)
 
         for q in range(4):
-            nc.scalar.dma_start(
+            nc.sync.dma_start(
                 tab_s[QUAD * q : QUAD * q + 2 * ROWS, :],
                 tab_scales[:, ROWS * q : ROWS * (q + 1), :].bitcast(I32),
             )
-        w1_raw = held([P, 2, H // 2], I32, "w1_raw", "slot_c")
+        w1_raw = placed([P, 2, H // 2], I32, "w1_raw", 8)
         nc.sync.dma_start(w1_raw[:], w1_words.rearrange("a p c -> p a c").bitcast(I32))
-        tab_w0 = held([P, T], I32, "tab_w0", "slot_b")
-        nc.sync.dma_start(tab_w0[:], tab_words[0].rearrange("p t i -> p (t i)").bitcast(I32))
+
+        def load_w2(g, kib):
+            raw = placed([P, PACK, BLOCK], F32, "w2_raw%d" % g, kib)
+            nc.sync.dma_start(raw[:], w2[:, g * BLOCK : (g + 1) * BLOCK].rearrange("(p j) c -> p j c", j=PACK))
+            return raw
+
+        w2_raw0 = load_w2(0, 0)
         for q in range(4):
-            nc.gpsimd.dma_start(
+            nc.scalar.dma_start(
                 w_s[QUAD * q : QUAD * q + ROWS, :, :],
                 w1_scales[:, ROWS * q : ROWS * (q + 1), :].rearrange("a r c -> r a c").bitcast(I32),
             )
         for q in range(4):
-            nc.gpsimd.dma_start(
+            nc.scalar.dma_start(
                 w_s[QUAD * q + ROWS : QUAD * q + 2 * ROWS, :, :],
                 w3_scales[:, ROWS * q : ROWS * (q + 1), :].rearrange("a r c -> r a c").bitcast(I32),
             )
         for q in range(4):
-            nc.scalar.dma_start(
+            nc.gpsimd.dma_start(
                 tab2_s[QUAD * q : QUAD * q + ROWS, :],
                 tab2_scales[0, ROWS * q : ROWS * (q + 1), :].bitcast(I32),
             )
-        gain_sb = held([P, 2, PACK], F32, "gain_sb")
-        nc.gpsimd.dma_start(gain_sb[:], gain.rearrange("(g p t) -> p g t", g=2, t=PACK))
 
-        v_s = held([P, S], U8, "v_s")
-        nc.vector.tensor_copy(v_s[:], tab_s[:].bitcast(U8).indirect(idx[:]))
-        for q in range(4):
-            nc.scalar.dma_start(
-                v_s1[QUAD * q : QUAD * q + ROWS, :],
-                v_s[QUAD * q + ROWS : QUAD * q + 2 * ROWS, :].bitcast(I32),
-            )
-        v_scale = [v_s[:], v_s1[:].bitcast(U8)]
-
-        tab_w1 = held([P, T], I32, "tab_w1", "slot_a")
-        nc.sync.dma_start(tab_w1[:], tab_words[1].rearrange("p t i -> p (t i)").bitcast(I32))
 
         w1_p = held([P, 2 * H], U16, "w1_p")
         nc.vector.tensor_copy(
             w1_p[:].rearrange("p (g t m) -> p g t m", t=PACK, m=P),
             w1_raw[:].rearrange("p a c -> p (a c)").bitcast(U16).rearrange("p (g m t) -> p g t m", t=PACK, m=P),
         )
-        v2_s = held([P, S], U8, "v2_s")
-        nc.vector.tensor_copy(v2_s[:], tab2_s[:].bitcast(U8).indirect(idx2[:]))
-
-        def load_w2(g, tag):
-            raw = held([P, PACK, BLOCK], F32, "w2_raw%d" % g, tag)
-            nc.sync.dma_start(raw[:], w2[:, g * BLOCK : (g + 1) * BLOCK].rearrange("(p j) c -> p j c", j=PACK))
-            return raw
-
-        w2_raw0 = load_w2(0, "slot_c")
+        tab_w0 = placed([P, T], I32, "tab_w0", 9)
+        nc.sync.dma_start(tab_w0[:], tab_words[0].rearrange("p t i -> p (t i)").bitcast(I32))
+        v_s = placed([P, S], U8, "v_s", 8)
+        nc.vector.tensor_copy(v_s[:], tab_s[:].bitcast(U8).indirect(idx[:]))
+        for q in range(4):
+            nc.sync.dma_start(
+                v_s1[QUAD * q : QUAD * q + ROWS, :],
+                v_s[QUAD * q + ROWS : QUAD * q + 2 * ROWS, :].bitcast(I32),
+            )
+        v_scale = [v_s[:], v_s1[:].bitcast(U8)]
+        tab_w1 = placed([P, T], I32, "tab_w1", 27)
+        nc.sync.dma_start(tab_w1[:], tab_words[1].rearrange("p t i -> p (t i)").bitcast(I32))
 
         v = {}
 
-        def gather_v(a, h, window):
-            v[a, h] = held([P, HALF], U32, "v%d%d" % (a, h))
+        def gather_v(a, h, window, kib=None):
+            name = "v%d%d" % (a, h)
+            v[a, h] = held([P, HALF], U32, name) if kib is None else placed([P, HALF], U32, name, kib)
             nc.vector.tensor_copy(v[a, h][:], window[:].bitcast(U32).indirect(half_of(idx, h)))
 
-        gather_v(0, 0, tab_w0)
-        gather_v(0, 1, tab_w0)
-        w_sp = held([P, 2 * H], U8, "w_sp")
+        w_sp = placed([P, 2 * H], U8, "w_sp", 25)
         nc.vector.tensor_copy(
             w_sp[:].rearrange("p (g t m) -> p g t m", t=PACK, m=P),
             w_s[:].rearrange("p a c -> p (a c)").bitcast(U8).rearrange("p (g m t) -> p g t m", t=PACK, m=P),
         )
-        tab2_w = held([P, T // 2], I32, "tab2_w", "slot_b")
+        tab2_w = placed([P, T // 2], I32, "tab2_w", 44)
         nc.sync.dma_start(tab2_w[:], tab2_words[0].bitcast(I32))
-        gather_v(1, 0, tab_w1)
-        gather_v(1, 1, tab_w1)
-        w2_raw1 = load_w2(1, "slot_a")
+        v2_s = placed([P, S], U8, "v2_s", 43)
+        nc.vector.tensor_copy(v2_s[:], tab2_s[:].bitcast(U8).indirect(idx2[:]))
 
         w2_q, w2_s = {}, {}
 
@@ -180,12 +180,12 @@ def tile_list_merge_negotiation_costs_kernel(
         a_sb = {}
 
         def make_a(g, h):
+            a_sb[g, h] = held([P, PACK, HALF], F32, "a%d%d" % (g, h))
             for t in range(PACK):
                 acc = bank("a_ps")
                 pass_a(acc[:], 0, g, t, h, whole, True, False)
                 pass_a(acc[:], 1, g, t, h, whole, False, True)
-                a_sb[g, t, h] = held([P, HALF], F32, "a%d%d%d" % (g, t, h))
-                nc.scalar.copy(a_sb[g, t, h][:], acc[:])
+                nc.scalar.copy(a_sb[g, h][:, t, :], acc[:])
 
         diff = {}
 
@@ -194,7 +194,7 @@ def tile_list_merge_negotiation_costs_kernel(
             for t in range(PACK):
                 acc = bank("b_ps")
                 pass_b(acc[:], g, t, h, whole, True, True)
-                nc.vector.tensor_tensor(diff[g, h][:, t, :], acc[:], a_sb[g, t, h][:], ALU.add)
+                nc.vector.tensor_tensor(diff[g, h][:, t, :], acc[:], a_sb[g, h][:, t, :], ALU.add)
 
         bounded = {}
 
@@ -230,99 +230,207 @@ def tile_list_merge_negotiation_costs_kernel(
             h_s[g, h] = held([P, HALF], U8, "h_s%d%d" % (g, h))
             nc.vector.quantize_mx(out=h_q[g, h][:].bitcast(FP8X4), scales=h_s[g, h][:], in_=h_bf[g, h][:])
 
-        def pass_c(acc, g, b, t, h, start, stop):
+        def make_split(g, h):
+            planes = work.tile([P, PACK, HALF], BF16, name="planes_half", tag="planes_half")
+            for t in range(PACK):
+                th = work.tile([P, HALF], F32, name="th_tile", tag="th_tile", bufs=4)
+                nc.scalar.activation(th[:], diff[g, h][:, t, :], ACT.Tanh, bias=no_bias[:])
+                nc.scalar.activation(planes[:, t, :], th[:], ACT.Copy, scale=gain_sb[:, g, t : t + 1])
+            bounded[g, h] = planes
+
+        def weave(g, h):
+            h_bf[g, h] = work.tile([P, HALF * PACK], BF16, name="h_bf", tag="h_bf", align_bytes=64)
+            nc.vector.tensor_copy(*woven(h_bf[g, h][:], bounded[g, h][:]))
+
+        def pass_c(acc, g, b, t, words, scales, start, stop):
             c = slice(g * H + cols(b, t).start, g * H + cols(b, t).stop)
             nc.tensor.matmul_mx(
                 out=acc, lhsT=w3_p[g][:, cols(b, t)].bitcast(FP8X4), lhsT_scale=w_sp[ROWS:P, c],
-                rhs=h_q[g, h][:].bitcast(FP8X4), rhs_scale=h_s[g, h][:], start=start, stop=stop,
+                rhs=words.bitcast(FP8X4), rhs_scale=scales, start=start, stop=stop,
             )
 
-        def store(b, t, h, res):
-            rows = out[b * BLOCK : (b + 1) * BLOCK, h * HALF : (h + 1) * HALF].rearrange("(p t) j -> p t j", t=PACK)
-            nc.sync.dma_start(rows[:, t, :], res[:])
+        def out_rows(b):
+            return out[b * BLOCK : (b + 1) * BLOCK, :].rearrange("(p t) j -> p t j", t=PACK)
 
         def result():
             return work.tile([P, HALF], F32, name="res", tag="res", bufs=8)
 
-        make_a(0, 0)
+        def woven(dst, src):
+            return dst.rearrange("p (c i t) -> p c t i", i=4, t=PACK), src.rearrange("p t (c i) -> p c t i", i=4)
+
+        def span(u):
+            return slice(u * QUARTER, (u + 1) * QUARTER)
+
+        late_diff, late_th, late_bf, late_q, late_s = {}, {}, {}, {}, {}
+
+        def diff_quarter(u):
+            late_diff[u] = work.tile([P, PACK, QUARTER], F32, name="late_diff", tag="late_diff")
+            for pair in range(2):
+                acc = bank("b_ps")
+                for s in range(2):
+                    pass_b(acc[:, span(s)], 0, 2 * pair + s, 1, span(u), True, True)
+                ts = slice(2 * pair, 2 * pair + 2)
+                nc.vector.tensor_tensor(
+                    late_diff[u][:, ts, :], acc[:].rearrange("p (s j) -> p s j", s=2), a_sb[0, 1][:, ts, span(u)], ALU.add
+                )
+
+        def tanh_quarter(u):
+            if ROUTE[u] != "v":
+                th = work.tile([P, PACK, QUARTER], F32, name="th_last", tag="th_last", bufs=3)
+                nc.scalar.activation(th[:], late_diff[u][:], ACT.Tanh, bias=no_bias[:])
+                planes = work.tile([P, PACK, QUARTER], BF16, name="planes", tag="planes", bufs=4)
+                for t in range(PACK):
+                    nc.scalar.activation(planes[:, t, :], th[:, t, :], ACT.Copy, scale=gain_sb[:, 0, t : t + 1])
+                late_th[u] = planes
+                return
+            late_th[u] = work.tile([P, QUARTER * PACK], F32, name="th", tag="th", bufs=4)
+            dst, src = woven(late_th[u][:], late_diff[u][:])
+            nc.scalar.activation(dst, src, ACT.Tanh, bias=no_bias[:])
+
+        def weigh_quarter(u):
+            late_bf[0, u] = work.tile([P, QUARTER * PACK], BF16, name="late_bf", tag="late_bf", bufs=4, align_bytes=64)
+            if ROUTE[u] == "v":
+                weigh(late_bf[0, u][:], late_th[u][:], 0, QUARTER)
+            elif ROUTE[u] == "p":
+                nc.vector.tensor_copy(*woven(late_bf[0, u][:], late_th[u][:]))
+            else:
+                nc.scalar.copy(*woven(late_bf[0, u][:], late_th[u][:]))
+
+        def make_last(u):
+            th = work.tile([P, PACK, QUARTER], F32, name="th_last", tag="th_last", bufs=3)
+            for c in range(QUARTER // CHUNK):
+                js = slice(u * QUARTER + c * CHUNK, u * QUARTER + (c + 1) * CHUNK)
+                acc = bank("d_ps")
+                for t in range(PACK):
+                    part = acc[:, t * CHUNK : (t + 1) * CHUNK]
+                    pass_a(part, 0, 1, t, 1, js, True, False)
+                    pass_a(part, 1, 1, t, 1, js, False, False)
+                    pass_b(part, 1, t, 1, js, False, True)
+                nc.scalar.activation(
+                    th[:, :, c * CHUNK : (c + 1) * CHUNK], acc[:].rearrange("p (t j) -> p t j", t=PACK),
+                    ACT.Tanh, bias=no_bias[:],
+                )
+            planes = work.tile([P, PACK, QUARTER], BF16, name="planes", tag="planes", bufs=4)
+            for t in range(PACK):
+                nc.scalar.activation(planes[:, t, :], th[:, t, :], ACT.Copy, scale=gain_sb[:, 1, t : t + 1])
+            late_bf[1, u] = work.tile([P, QUARTER * PACK], BF16, name="late_bf", tag="late_bf", bufs=4, align_bytes=64)
+            nc.scalar.copy(*woven(late_bf[1, u][:], planes[:]))
+
+        def quantize_quarter(g, u):
+            late_q[g, u] = held([P, QUARTER], U32, "late_q%d%d" % (g, u))
+            late_s[g, u] = held([P, QUARTER], U8, "late_s%d%d" % (g, u))
+            nc.vector.quantize_mx(out=late_q[g, u][:].bitcast(FP8X4), scales=late_s[g, u][:], in_=late_bf[g, u][:])
+
+        def finish_first_half(b, t):
+            acc = bank("c_ps")
+            pass_c(acc[:], 0, b, t, h_q[0, 0][:], h_s[0, 0][:], True, False)
+            pass_c(acc[:], 1, b, t, h_q[1, 0][:], h_s[1, 0][:], False, True)
+            res = result()
+            nc.vector.tensor_tensor(res[:], acc[:], a_sb[b, 0][:, t, :], ALU.add)
+            nc.sync.dma_start(out_rows(b)[:, t, 0:HALF], res[:])
+
+        opened = {}
+
+        def open_residual(u):
+            for pair in range(2):
+                acc = bank("c_ps")
+                opened[u, pair, 1] = acc
+                for s in range(2):
+                    for a in range(2):
+                        for c in range(QUARTER // CHUNK):
+                            lo = c * CHUNK
+                            part = acc[:, s * QUARTER + lo : s * QUARTER + lo + CHUNK]
+                            js = slice(u * QUARTER + lo, u * QUARTER + lo + CHUNK)
+                            pass_a(part, a, 1, 2 * pair + s, 1, js, (s, a, c) == (0, 0, 0), False)
+
+        def open_costs(u):
+            for pair in range(2):
+                for b in (1, 0):
+                    if b == 0:
+                        opened[u, pair, 0] = bank("c_ps")
+                    for s in range(2):
+                        pass_c(
+                            opened[u, pair, b][:, span(s)], 0, b, 2 * pair + s, late_q[0, u][:], late_s[0, u][:],
+                            b == 0 and s == 0, False,
+                        )
+
+        def finish_quarter(u):
+            for pair in range(2):
+                ts = slice(2 * pair, 2 * pair + 2)
+                for b in (1, 0):
+                    acc = opened[u, pair, b]
+                    for s in range(2):
+                        pass_c(acc[:, span(s)], 1, b, 2 * pair + s, late_q[1, u][:], late_s[1, u][:], False, s == 1)
+                    res = result()
+                    two = res[:].rearrange("p (s j) -> p s j", s=2)
+                    if b == 0:
+                        nc.vector.tensor_tensor(two, acc[:].rearrange("p (s j) -> p s j", s=2), a_sb[0, 1][:, ts, span(u)], ALU.add)
+                    else:
+                        nc.scalar.copy(res[:], acc[:])
+                    nc.sync.dma_start(out_rows(b)[:, ts, HALF + u * QUARTER : HALF + (u + 1) * QUARTER], two)
+
         grouped0, dst0, src0 = w2_views(0, w2_raw0)
-        nc.vector.tensor_scalar(dst0, src0, -1.0, None, ALU.mult)
-        w3_raw = held([P, 2, H], I32, "w3_raw", "slot_c")
-        nc.sync.dma_start(w3_raw[:], w3_words.rearrange("a p c i -> p a (c i)").bitcast(I32))
-        gather_v2(0)
+        w3_p = []
+
+        def reorder_w3():
+            for g in range(2):
+                w3_p.append(held([P, H], U32, "w3_p%d" % g))
+                nc.vector.tensor_copy(
+                    w3_p[g][:].rearrange("p (b t c i) -> p b c t i", t=PACK, i=4, b=2),
+                    w3_raw[:, g, :].bitcast(U32).rearrange("p (b c i t) -> p b c t i", t=PACK, i=4, b=2),
+                )
+
+        nc.scalar.activation(dst0, src0, ACT.Copy, scale=-1.0)
         quantize_w2(0, grouped0)
-        make_a(0, 1)
+        gather_v(0, 0, tab_w0)
+        gather_v(0, 1, tab_w0)
+        w2_raw1 = load_w2(1, 9)
+        gain_sb = placed([P, 2, PACK], F32, "gain_sb", 17)
+        nc.sync.dma_start(gain_sb[:], gain.rearrange("(g p t) -> p g t", g=2, t=PACK))
+        gather_v(1, 0, tab_w1)
+        gather_v(1, 1, tab_w1)
+        w3_raw = placed([P, 2, H], I32, "w3_raw", 27)
+        nc.sync.dma_start(w3_raw[:], w3_words.rearrange("a p c i -> p a (c i)").bitcast(I32))
+        make_a(0, 0)
+        make_a(1, 0)
+        gather_v2(0)
         make_diff(0, 0)
         gather_v2(1)
-        make_tanh(0, 0)
-        make_a(1, 0)
-        make_diff(0, 1)
         grouped1, dst1, src1 = w2_views(1, w2_raw1)
-        nc.scalar.activation(dst1, src1, ACT.Copy, scale=-1.0)
-        make_h(0, 0)
-        make_tanh(0, 1)
+        nc.vector.tensor_scalar(dst1, src1, -1.0, None, ALU.mult)
+        make_tanh(0, 0)
         quantize_w2(1, grouped1)
-        quantize_h(0, 0)
+        make_a(0, 1)
         make_diff(1, 0)
-        make_h(0, 1)
+        reorder_w3()
+        make_h(0, 0)
         make_tanh(1, 0)
-        w3_p = []
-        for g in range(2):
-            w3_p.append(held([P, H], U32, "w3_p%d" % g))
-            nc.vector.tensor_copy(
-                w3_p[g][:].rearrange("p (b t c i) -> p b c t i", t=PACK, i=4, b=2),
-                w3_raw[:, g, :].bitcast(U32).rearrange("p (b c i t) -> p b c t i", t=PACK, i=4, b=2),
-            )
-        quantize_h(0, 1)
-
-        last = []
-        for c in range(HALF // CHUNK):
-            js = slice(c * CHUNK, (c + 1) * CHUNK)
-            acc = bank("d_ps")
-            for t in range(PACK):
-                part = acc[:, t * CHUNK : (t + 1) * CHUNK]
-                pass_a(part, 0, 1, t, 1, js, True, False)
-                pass_a(part, 1, 1, t, 1, js, False, False)
-                pass_b(part, 1, t, 1, js, False, True)
-            th = work.tile([P, CHUNK * PACK], F32, name="th_last", tag="th_last", bufs=4)
-            nc.scalar.activation(
-                th[:].rearrange("p (j t) -> p j t", t=PACK), acc[:].rearrange("p (t j) -> p j t", t=PACK),
-                ACT.Tanh, bias=no_bias[:],
-            )
-            last.append(th)
+        quantize_h(0, 0)
+        diff_quarter(0)
         make_h(1, 0)
+        tanh_quarter(0)
         quantize_h(1, 0)
-
-        h_bf[1, 1] = work.tile([P, HALF * PACK], BF16, name="h_bf", tag="h_bf", align_bytes=64)
-        for c in range(HALF // CHUNK):
-            weigh(h_bf[1, 1][:, c * CHUNK * PACK : (c + 1) * CHUNK * PACK], last[c][:], 1, CHUNK)
-        for b in range(2):
-            for t in range(PACK):
-                acc = bank("c_ps")
-                pass_c(acc[:], 0, b, t, 0, True, False)
-                pass_c(acc[:], 1, b, t, 0, False, True)
-                res = result()
-                nc.vector.tensor_tensor(res[:], acc[:], a_sb[b, t, 0][:], ALU.add)
-                store(b, t, 0, res)
-                if (b, t) == (0, 0):
-                    quantize_h(1, 1)
-
-        open_banks = {}
-        for t in range(PACK):
-            acc = bank("c_ps")
-            pass_a(acc[:], 0, 1, t, 1, whole, True, False)
-            pass_a(acc[:], 1, 1, t, 1, whole, False, False)
-            pass_c(acc[:], 0, 1, t, 1, False, False)
-            open_banks[1, t] = acc
-        for t in range(PACK):
-            acc = bank("c_ps")
-            pass_c(acc[:], 0, 0, t, 1, True, False)
-            pass_c(acc[:], 1, 0, t, 1, False, True)
-            res = result()
-            nc.vector.tensor_tensor(res[:], acc[:], a_sb[0, t, 1][:], ALU.add)
-            store(0, t, 1, res)
-            acc = open_banks[1, t]
-            pass_c(acc[:], 1, 1, t, 1, False, True)
-            res = result()
-            nc.scalar.copy(res[:], acc[:])
-            store(1, t, 1, res)
+        diff_quarter(1)
+        make_last(0)
+        tanh_quarter(1)
+        weigh_quarter(0)
+        finish_first_half(0, 0)
+        quantize_quarter(0, 0)
+        finish_first_half(0, 1)
+        quantize_quarter(1, 0)
+        make_last(1)
+        open_residual(0)
+        finish_first_half(0, 2)
+        finish_first_half(0, 3)
+        open_costs(0)
+        finish_first_half(1, 0)
+        finish_quarter(0)
+        finish_first_half(1, 1)
+        weigh_quarter(1)
+        finish_first_half(1, 2)
+        open_residual(1)
+        quantize_quarter(0, 1)
+        finish_first_half(1, 3)
+        open_costs(1)
+        quantize_quarter(1, 1)
+        finish_quarter(1)

@@ -18,13 +18,13 @@ ACT = mybir.ActivationFunctionType
 
 P = 128
 PACK = 4
-BLOCK = P * PACK
+GROUP = P * PACK
 HALF = 512
 QUARTER = 256
 CHUNK = 128
-ROUTE = "vp"
 QUAD = 32
 ROWS = 4
+RUN = 4
 
 
 def tile_list_merge_negotiation_costs_kernel(
@@ -39,8 +39,8 @@ def tile_list_merge_negotiation_costs_kernel(
         work = ctx.enter_context(tc.tile_pool(name="work", bufs=2))
         psum = ctx.enter_context(tc.psum_pool(name="psum", bufs=8))
 
-        def held(shape, dtype, name, tag=None):
-            return keep.tile(shape, dtype, name=name, tag=tag or name, align_bytes=64)
+        def held(shape, dtype, name):
+            return keep.tile(shape, dtype, name=name, tag=name, align_bytes=64)
 
         def placed(shape, dtype, name, kib):
             return shared.tile(shape, dtype, name=name, tag=name, align_bytes=64, offset=kib * 1024)
@@ -48,136 +48,160 @@ def tile_list_merge_negotiation_costs_kernel(
         def bank(name):
             return psum.tile([P, HALF], F32, name=name, tag="bank")
 
+        def span(n, width):
+            return slice(n * width, (n + 1) * width)
+
         idx = lists.tile([P, S // 16], U16, name="idx")
         idx2 = lists.tile([P, S // 16], U16, name="idx2")
         nc.sync.dma_start(idx[:], offs)
         nc.sync.dma_start(idx2[:], offs2)
 
-        def half_of(index_tile, h):
-            return index_tile[:, h * (HALF // 16) : (h + 1) * (HALF // 16)]
-
-        tab_s = placed([P, T // 4], I32, "tab_s", 25)
-        v_s1 = held([P, S // 4], I32, "v_s1")
-        w_s = placed([P, 2, H // 4], I32, "w_s", 43)
-        tab2_s = held([P, T // 4], I32, "tab2_s")
+        w1_raw = placed([P, 2, H // 2], I32, "w1_raw", 16)
+        nc.sync.dma_start(w1_raw[:], w1_words.rearrange("a p c -> p a c").bitcast(I32))
+        tab_s = placed([P, T // 4], I32, "tab_s", 35)
+        v_planes = held([P, 2, S // 4], I32, "v_planes")
+        v2_plane = held([P, S // 4], I32, "v2_plane")
+        w_s = held([P, 2, H // 4], I32, "w_s")
+        tab2_s = placed([P, T // 4], I32, "tab2_s", 45)
         zero = placed([P, 1], F32, "zero", 0)
         no_bias = held([P, 1], F32, "no_bias")
         nc.vector.memset(tab_s[:, 0 : T // 8], 0)
         nc.gpsimd.memset(tab_s[:, T // 8 : T // 4], 0)
-        nc.gpsimd.memset(v_s1[:], 0)
         nc.vector.memset(zero[:], 0.0)
-        nc.vector.memset(w_s[:], 0)
         nc.vector.memset(tab2_s[:], 0)
+        nc.vector.memset(w_s[:], 0)
+        nc.vector.memset(v_planes[:], 0)
+        nc.vector.memset(v2_plane[:], 0)
         nc.scalar.activation(no_bias[:], zero[:], ACT.Tanh)
 
-        for q in range(4):
-            nc.sync.dma_start(
-                tab_s[QUAD * q : QUAD * q + 2 * ROWS, :],
-                tab_scales[:, ROWS * q : ROWS * (q + 1), :].bitcast(I32),
-            )
-        w1_raw = placed([P, 2, H // 2], I32, "w1_raw", 8)
-        nc.sync.dma_start(w1_raw[:], w1_words.rearrange("a p c -> p a c").bitcast(I32))
+        tab_step, tab2_step, tab2_first = P // 32, P // 16, ROWS
+        nc.sync.dma_start(tab_s[0:P:tab_step, :], tab_scales.rearrange("a q t -> (a q) t").bitcast(I32))
+        nc.sync.dma_start(tab2_s[tab2_first:P:tab2_step, :], tab2_scales[0].bitcast(I32))
+        for first, scales in ((0, w1_scales), (ROWS, w3_scales)):
+            for q in range(P // QUAD):
+                nc.sync.dma_start(
+                    w_s[QUAD * q + first : QUAD * q + first + ROWS, :, :],
+                    scales[:, span(q, ROWS), :].rearrange("a r c -> r a c").bitcast(I32),
+                )
+
+        def load_table_pass(a, kib):
+            words = placed([P, T], I32, "tab_w%d" % a, kib)
+            nc.sync.dma_start(words[:], tab_words[a].rearrange("p t i -> p (t i)").bitcast(I32))
+            return words
 
         def load_w2(g, kib):
-            raw = placed([P, PACK, BLOCK], F32, "w2_raw%d" % g, kib)
-            nc.sync.dma_start(raw[:], w2[:, g * BLOCK : (g + 1) * BLOCK].rearrange("(p j) c -> p j c", j=PACK))
+            raw = placed([P, PACK, GROUP], F32, "w2_raw%d" % g, kib)
+            nc.sync.dma_start(raw[:], w2[:, span(g, GROUP)].rearrange("(p j) c -> p j c", j=PACK))
             return raw
 
-        w2_raw0 = load_w2(0, 0)
-        for q in range(4):
-            nc.scalar.dma_start(
-                w_s[QUAD * q : QUAD * q + ROWS, :, :],
-                w1_scales[:, ROWS * q : ROWS * (q + 1), :].rearrange("a r c -> r a c").bitcast(I32),
-            )
-        for q in range(4):
-            nc.scalar.dma_start(
-                w_s[QUAD * q + ROWS : QUAD * q + 2 * ROWS, :, :],
-                w3_scales[:, ROWS * q : ROWS * (q + 1), :].rearrange("a r c -> r a c").bitcast(I32),
-            )
-        for q in range(4):
-            nc.gpsimd.dma_start(
-                tab2_s[QUAD * q : QUAD * q + ROWS, :],
-                tab2_scales[0, ROWS * q : ROWS * (q + 1), :].bitcast(I32),
+        def reorder_columns(dst, src):
+            nc.vector.tensor_copy(
+                dst.rearrange("p (g t m) -> p g t m", t=PACK, m=P),
+                src.rearrange("p (g m t) -> p g t m", t=PACK, m=P),
             )
 
+        def move_rows(plane, gathered, first, step):
+            for q in range(P // QUAD):
+                lo = first + step * ROWS * q
+                nc.sync.dma_start(
+                    plane[QUAD * q : QUAD * q + ROWS, :],
+                    gathered[lo : lo + step * (ROWS - 1) + 1 : step, :].bitcast(I32),
+                )
 
+        tab_w0 = load_table_pass(0, 0)
         w1_p = held([P, 2 * H], U16, "w1_p")
-        nc.vector.tensor_copy(
-            w1_p[:].rearrange("p (g t m) -> p g t m", t=PACK, m=P),
-            w1_raw[:].rearrange("p a c -> p (a c)").bitcast(U16).rearrange("p (g m t) -> p g t m", t=PACK, m=P),
-        )
-        tab_w0 = placed([P, T], I32, "tab_w0", 9)
-        nc.sync.dma_start(tab_w0[:], tab_words[0].rearrange("p t i -> p (t i)").bitcast(I32))
-        v_s = placed([P, S], U8, "v_s", 8)
-        nc.vector.tensor_copy(v_s[:], tab_s[:].bitcast(U8).indirect(idx[:]))
-        for q in range(4):
-            nc.sync.dma_start(
-                v_s1[QUAD * q : QUAD * q + ROWS, :],
-                v_s[QUAD * q + ROWS : QUAD * q + 2 * ROWS, :].bitcast(I32),
-            )
-        v_scale = [v_s[:], v_s1[:].bitcast(U8)]
-        tab_w1 = placed([P, T], I32, "tab_w1", 27)
-        nc.sync.dma_start(tab_w1[:], tab_words[1].rearrange("p t i -> p (t i)").bitcast(I32))
+        reorder_columns(w1_p[:], w1_raw[:].rearrange("p a c -> p (a c)").bitcast(U16))
 
-        v = {}
+        v_rows = placed([P, S], U8, "v_rows", 16)
+        nc.vector.tensor_copy(v_rows[:], tab_s[:].bitcast(U8).indirect(idx[:]))
+        move_rows(v_planes[:, 0, :], v_rows, 0, tab_step)
+        tab_w1 = load_table_pass(1, 20)
+        move_rows(v_planes[:, 1, :], v_rows, 16 * tab_step, tab_step)
 
-        def gather_v(a, h, window, kib=None):
-            name = "v%d%d" % (a, h)
-            v[a, h] = held([P, HALF], U32, name) if kib is None else placed([P, HALF], U32, name, kib)
-            nc.vector.tensor_copy(v[a, h][:], window[:].bitcast(U32).indirect(half_of(idx, h)))
-
-        w_sp = placed([P, 2 * H], U8, "w_sp", 25)
-        nc.vector.tensor_copy(
-            w_sp[:].rearrange("p (g t m) -> p g t m", t=PACK, m=P),
-            w_s[:].rearrange("p a c -> p (a c)").bitcast(U8).rearrange("p (g m t) -> p g t m", t=PACK, m=P),
-        )
-        tab2_w = placed([P, T // 2], I32, "tab2_w", 44)
+        v2_rows = placed([P, S], U8, "v2_rows", 36)
+        nc.vector.tensor_copy(v2_rows[:], tab2_s[:].bitcast(U8).indirect(idx2[:]))
+        w2_raw0 = load_w2(0, 39)
+        tab2_w = placed([P, T // 2], I32, "tab2_w", 47)
         nc.sync.dma_start(tab2_w[:], tab2_words[0].bitcast(I32))
-        v2_s = placed([P, S], U8, "v2_s", 43)
-        nc.vector.tensor_copy(v2_s[:], tab2_s[:].bitcast(U8).indirect(idx2[:]))
+        move_rows(v2_plane, v2_rows, tab2_first, tab2_step)
 
-        w2_q, w2_s = {}, {}
+        w_planes = placed([P, 2 * H], U8, "w_planes", 37)
+        reorder_columns(w_planes[:], w_s[:].rearrange("p a c -> p (a c)").bitcast(U8))
 
-        def w2_views(g, raw):
-            grouped = held([P, PACK * BLOCK], BF16, "w2_bf%d" % g)
-            return (
-                grouped,
-                grouped[:].rearrange("p (t m j) -> p m j t", t=PACK, j=PACK),
-                raw[:].rearrange("p j (m t) -> p m j t", t=PACK),
-            )
+        v, v2 = {}, {}
 
-        def quantize_w2(g, grouped):
-            w2_q[g] = held([P, BLOCK], U32, "w2_q%d" % g)
-            w2_s[g] = held([P, BLOCK], U8, "w2_s%d" % g)
-            nc.vector.quantize_mx(out=w2_q[g][:].bitcast(FP8X4), scales=w2_s[g][:], in_=grouped[:])
-
-        def cols(g, t):
-            return slice(g * BLOCK + t * P, g * BLOCK + (t + 1) * P)
-
-        def pass_a(acc, a, g, t, h, js, start, stop):
-            c = slice(a * H + cols(g, t).start, a * H + cols(g, t).stop)
-            sj = slice(h * HALF + js.start, h * HALF + js.stop)
-            nc.tensor.matmul_mx(
-                out=acc, lhsT=w1_p[:, c].bitcast(FP4X4), lhsT_scale=w_sp[:, c],
-                rhs=v[a, h][:, js].bitcast(FP8X4), rhs_scale=v_scale[a][:, sj], start=start, stop=stop,
-            )
-
-        v2 = {}
+        def gather_v(a, h, window):
+            v[a, h] = held([P, HALF], U32, "v%d%d" % (a, h))
+            nc.vector.tensor_copy(v[a, h][:], window[:].bitcast(U32).indirect(idx[:, span(h, HALF // 16)]))
 
         def gather_v2(h):
             v2[h] = held([P, HALF], U16, "v2%d" % h)
-            nc.vector.tensor_copy(v2[h][:], tab2_w[:].bitcast(U16).indirect(half_of(idx2, h)))
+            nc.vector.tensor_copy(v2[h][:], tab2_w[:].bitcast(U16).indirect(idx2[:, span(h, HALF // 16)]))
 
-        def pass_b(acc, g, t, h, js, start, stop):
-            c = cols(0, t)
-            sj = slice(h * HALF + js.start, h * HALF + js.stop)
-            nc.tensor.matmul_mx(
-                out=acc, lhsT=w2_q[g][:, c].bitcast(FP8X4), lhsT_scale=w2_s[g][:, c],
-                rhs=v2[h][:, js].bitcast(FP4X4), rhs_scale=v2_s[:, sj], start=start, stop=stop,
+        w2_bf, w2_q, w2_s = {}, {}, {}
+
+        def round_w2(g, raw):
+            w2_bf[g] = held([P, PACK * GROUP], BF16, "w2_bf%d" % g)
+            nc.vector.tensor_scalar(
+                w2_bf[g][:].rearrange("p (t m j) -> p m j t", t=PACK, j=PACK),
+                raw[:].rearrange("p j (m t) -> p m j t", t=PACK),
+                -1.0, None, ALU.mult,
             )
 
-        whole = slice(0, HALF)
-        a_sb = {}
+        def quantize(values, width, name):
+            words = held([P, width], U32, name + "_q")
+            plane = held([P, width], U8, name + "_s")
+            nc.vector.quantize_mx(out=words[:].bitcast(FP8X4), scales=plane[:], in_=values[:])
+            return words, plane
+
+        def quantize_w2(g):
+            w2_q[g], w2_s[g] = quantize(w2_bf[g], GROUP, "w2_%d" % g)
+
+        w3_p = []
+
+        def reorder_w3(raw):
+            for g in range(2):
+                w3_p.append(held([P, H], U32, "w3_p%d" % g))
+                nc.vector.tensor_copy(
+                    w3_p[g][:].rearrange("p (b t c i) -> p b c t i", t=PACK, i=RUN, b=2),
+                    raw[:, g, :].bitcast(U32).rearrange("p (b c i t) -> p b c t i", t=PACK, i=RUN, b=2),
+                )
+
+        def pass_a(acc, a, g, t, h, js, start, stop):
+            cols = span((a * H + g * GROUP) // P + t, P)
+            entries = slice(h * HALF + js.start, h * HALF + js.stop)
+            nc.tensor.matmul_mx(
+                out=acc, lhsT=w1_p[:, cols].bitcast(FP4X4), lhsT_scale=w_planes[:, cols],
+                rhs=v[a, h][:, js].bitcast(FP8X4), rhs_scale=v_planes[:, a, :].bitcast(U8)[:, entries],
+                start=start, stop=stop,
+            )
+
+        def pass_b(acc, g, t, h, js, start, stop):
+            entries = slice(h * HALF + js.start, h * HALF + js.stop)
+            nc.tensor.matmul_mx(
+                out=acc, lhsT=w2_q[g][:, span(t, P)].bitcast(FP8X4), lhsT_scale=w2_s[g][:, span(t, P)],
+                rhs=v2[h][:, js].bitcast(FP4X4), rhs_scale=v2_plane[:].bitcast(U8)[:, entries],
+                start=start, stop=stop,
+            )
+
+        def pass_cost(acc, g, b, t, h_words, h_plane, start, stop):
+            nc.tensor.matmul_mx(
+                out=acc, lhsT=w3_p[g][:, span(b * PACK + t, P)].bitcast(FP8X4),
+                lhsT_scale=w_planes[ROWS:P, span((g * H + b * GROUP) // P + t, P)],
+                rhs=h_words[:].bitcast(FP8X4), rhs_scale=h_plane[:], start=start, stop=stop,
+            )
+
+        def woven(dst, src):
+            return (
+                dst.rearrange("p (c i t) -> p c t i", i=RUN, t=PACK),
+                src.rearrange("p t (c i) -> p c t i", i=RUN),
+            )
+
+        def pairs(acc):
+            return acc.rearrange("p (s j) -> p s j", s=2)
+
+        whole = span(0, HALF)
+        a_sb, diff, h_bf, h_q = {}, {}, {}, {}
 
         def make_a(g, h):
             a_sb[g, h] = held([P, PACK, HALF], F32, "a%d%d" % (g, h))
@@ -187,149 +211,91 @@ def tile_list_merge_negotiation_costs_kernel(
                 pass_a(acc[:], 1, g, t, h, whole, False, True)
                 nc.scalar.copy(a_sb[g, h][:, t, :], acc[:])
 
-        diff = {}
+        def tanh_woven(src):
+            th = work.tile([P, QUARTER * PACK], F32, name="th", tag="th", bufs=3)
+            dst, tiles = woven(th[:], src)
+            nc.scalar.activation(dst, tiles, ACT.Tanh, bias=no_bias[:])
+            return th
 
-        def make_diff(g, h):
-            diff[g, h] = work.tile([P, PACK, HALF], F32, name="diff", tag="diff")
-            for t in range(PACK):
-                acc = bank("b_ps")
-                pass_b(acc[:], g, t, h, whole, True, True)
-                nc.vector.tensor_tensor(diff[g, h][:, t, :], acc[:], a_sb[g, h][:, t, :], ALU.add)
-
-        bounded = {}
-
-        def make_tanh(g, h):
-            for u in range(2):
-                th = work.tile([P, (HALF // 2) * PACK], F32, name="th", tag="th", bufs=4)
-                bounded[g, h, u] = th
-                js = slice(u * (HALF // 2), (u + 1) * (HALF // 2))
-                nc.scalar.activation(
-                    th[:].rearrange("p (c i t) -> p c t i", i=4, t=PACK),
-                    diff[g, h][:, :, js].rearrange("p t (c i) -> p c t i", i=4),
-                    ACT.Tanh, bias=no_bias[:],
-                )
-
-        h_q, h_s = {}, {}
-
-        def weigh(dst, th, g, n):
+        def weigh(dst, th, g):
             nc.vector.tensor_tensor(
-                dst.rearrange("p (j t) -> p j t", t=PACK), th.rearrange("p (j t) -> p j t", t=PACK),
-                gain_sb[:, g : g + 1, :].to_broadcast([P, n, PACK]), ALU.mult,
+                dst.rearrange("p (j t) -> p j t", t=PACK), th[:].rearrange("p (j t) -> p j t", t=PACK),
+                gain_sb[:, g : g + 1, :].to_broadcast([P, QUARTER, PACK]), ALU.mult,
             )
 
-        h_bf = {}
+        def scale_tile(dst, th, g, t):
+            nc.scalar.activation(dst, th, ACT.Copy, scale=gain_sb[:, g, t : t + 1])
 
-        def make_h(g, h):
-            h_bf[g, h] = work.tile([P, HALF * PACK], BF16, name="h_bf", tag="h_bf", align_bytes=64)
-            for u in range(2):
-                n = HALF // 2
-                weigh(h_bf[g, h][:, u * n * PACK : (u + 1) * n * PACK], bounded[g, h, u][:], g, n)
-
-        def quantize_h(g, h):
-            h_q[g, h] = held([P, HALF], U32, "h_q%d%d" % (g, h))
-            h_s[g, h] = held([P, HALF], U8, "h_s%d%d" % (g, h))
-            nc.vector.quantize_mx(out=h_q[g, h][:].bitcast(FP8X4), scales=h_s[g, h][:], in_=h_bf[g, h][:])
-
-        def make_split(g, h):
-            planes = work.tile([P, PACK, HALF], BF16, name="planes_half", tag="planes_half")
+        def scale_tiles(th, g):
+            tiles = work.tile([P, PACK, QUARTER], BF16, name="tiles", tag="tiles", bufs=4)
             for t in range(PACK):
-                th = work.tile([P, HALF], F32, name="th_tile", tag="th_tile", bufs=4)
-                nc.scalar.activation(th[:], diff[g, h][:, t, :], ACT.Tanh, bias=no_bias[:])
-                nc.scalar.activation(planes[:, t, :], th[:], ACT.Copy, scale=gain_sb[:, g, t : t + 1])
-            bounded[g, h] = planes
-
-        def weave(g, h):
-            h_bf[g, h] = work.tile([P, HALF * PACK], BF16, name="h_bf", tag="h_bf", align_bytes=64)
-            nc.vector.tensor_copy(*woven(h_bf[g, h][:], bounded[g, h][:]))
-
-        def pass_c(acc, g, b, t, words, scales, start, stop):
-            c = slice(g * H + cols(b, t).start, g * H + cols(b, t).stop)
-            nc.tensor.matmul_mx(
-                out=acc, lhsT=w3_p[g][:, cols(b, t)].bitcast(FP8X4), lhsT_scale=w_sp[ROWS:P, c],
-                rhs=words.bitcast(FP8X4), rhs_scale=scales, start=start, stop=stop,
-            )
+                scale_tile(tiles[:, t, :], th[:, t, :], g, t)
+            return tiles
 
         def out_rows(b):
-            return out[b * BLOCK : (b + 1) * BLOCK, :].rearrange("(p t) j -> p t j", t=PACK)
+            return out[span(b, GROUP), :].rearrange("(p t) j -> p t j", t=PACK)
 
         def result():
             return work.tile([P, HALF], F32, name="res", tag="res", bufs=8)
 
-        def woven(dst, src):
-            return dst.rearrange("p (c i t) -> p c t i", i=4, t=PACK), src.rearrange("p t (c i) -> p c t i", i=4)
+        def diff_half(g):
+            diff[g] = work.tile([P, PACK, HALF], F32, name="diff", tag="diff")
+            for t in range(PACK):
+                acc = bank("b_ps")
+                pass_b(acc[:], g, t, 0, whole, True, True)
+                nc.vector.tensor_tensor(diff[g][:, t, :], acc[:], a_sb[g, 0][:, t, :], ALU.add)
 
-        def span(u):
-            return slice(u * QUARTER, (u + 1) * QUARTER)
+        def half_bf(g):
+            h_bf[g] = work.tile([P, HALF * PACK], BF16, name="h_bf", tag="h_bf", align_bytes=64)
+            return h_bf[g]
 
-        late_diff, late_th, late_bf, late_q, late_s = {}, {}, {}, {}, {}
+        def quantize_half(g):
+            h_q[g] = quantize(h_bf[g], HALF, "h%d" % g)
+
+        def finish_half(b, t):
+            acc = bank("c_ps")
+            pass_cost(acc[:], 0, b, t, *h_q[0], True, False)
+            pass_cost(acc[:], 1, b, t, *h_q[1], False, True)
+            res = result()
+            nc.vector.tensor_tensor(res[:], acc[:], a_sb[b, 0][:, t, :], ALU.add)
+            nc.sync.dma_start(out_rows(b)[:, t, 0:HALF], res[:])
+
+        late_diff, late_bf, late_q, opened = {}, {}, {}, {}
 
         def diff_quarter(u):
             late_diff[u] = work.tile([P, PACK, QUARTER], F32, name="late_diff", tag="late_diff")
             for pair in range(2):
                 acc = bank("b_ps")
                 for s in range(2):
-                    pass_b(acc[:, span(s)], 0, 2 * pair + s, 1, span(u), True, True)
-                ts = slice(2 * pair, 2 * pair + 2)
-                nc.vector.tensor_tensor(
-                    late_diff[u][:, ts, :], acc[:].rearrange("p (s j) -> p s j", s=2), a_sb[0, 1][:, ts, span(u)], ALU.add
-                )
+                    pass_b(acc[:, span(s, QUARTER)], 0, 2 * pair + s, 1, span(u, QUARTER), True, True)
+                ts = span(pair, 2)
+                nc.vector.tensor_tensor(late_diff[u][:, ts, :], pairs(acc[:]), a_sb[0, 1][:, ts, span(u, QUARTER)], ALU.add)
 
-        def tanh_quarter(u):
-            if ROUTE[u] != "v":
-                th = work.tile([P, PACK, QUARTER], F32, name="th_last", tag="th_last", bufs=3)
-                nc.scalar.activation(th[:], late_diff[u][:], ACT.Tanh, bias=no_bias[:])
-                planes = work.tile([P, PACK, QUARTER], BF16, name="planes", tag="planes", bufs=4)
-                for t in range(PACK):
-                    nc.scalar.activation(planes[:, t, :], th[:, t, :], ACT.Copy, scale=gain_sb[:, 0, t : t + 1])
-                late_th[u] = planes
-                return
-            late_th[u] = work.tile([P, QUARTER * PACK], F32, name="th", tag="th", bufs=4)
-            dst, src = woven(late_th[u][:], late_diff[u][:])
-            nc.scalar.activation(dst, src, ACT.Tanh, bias=no_bias[:])
+        def quarter_bf(g, u):
+            late_bf[g, u] = work.tile([P, QUARTER * PACK], BF16, name="late_bf", tag="late_bf", bufs=4, align_bytes=64)
+            return late_bf[g, u]
 
-        def weigh_quarter(u):
-            late_bf[0, u] = work.tile([P, QUARTER * PACK], BF16, name="late_bf", tag="late_bf", bufs=4, align_bytes=64)
-            if ROUTE[u] == "v":
-                weigh(late_bf[0, u][:], late_th[u][:], 0, QUARTER)
-            elif ROUTE[u] == "p":
-                nc.vector.tensor_copy(*woven(late_bf[0, u][:], late_th[u][:]))
-            else:
-                nc.scalar.copy(*woven(late_bf[0, u][:], late_th[u][:]))
+        def plain_tanh_tile():
+            return work.tile([P, PACK, QUARTER], F32, name="th_plain", tag="th_plain", bufs=3)
 
-        def make_last(u):
-            th = work.tile([P, PACK, QUARTER], F32, name="th_last", tag="th_last", bufs=3)
+        def group1_quarter(u):
+            th = plain_tanh_tile()
             for c in range(QUARTER // CHUNK):
-                js = slice(u * QUARTER + c * CHUNK, u * QUARTER + (c + 1) * CHUNK)
+                js = span(u * (QUARTER // CHUNK) + c, CHUNK)
                 acc = bank("d_ps")
                 for t in range(PACK):
-                    part = acc[:, t * CHUNK : (t + 1) * CHUNK]
+                    part = acc[:, span(t, CHUNK)]
                     pass_a(part, 0, 1, t, 1, js, True, False)
                     pass_a(part, 1, 1, t, 1, js, False, False)
                     pass_b(part, 1, t, 1, js, False, True)
                 nc.scalar.activation(
-                    th[:, :, c * CHUNK : (c + 1) * CHUNK], acc[:].rearrange("p (t j) -> p t j", t=PACK),
-                    ACT.Tanh, bias=no_bias[:],
+                    th[:, :, span(c, CHUNK)], acc[:].rearrange("p (t j) -> p t j", t=PACK), ACT.Tanh, bias=no_bias[:]
                 )
-            planes = work.tile([P, PACK, QUARTER], BF16, name="planes", tag="planes", bufs=4)
-            for t in range(PACK):
-                nc.scalar.activation(planes[:, t, :], th[:, t, :], ACT.Copy, scale=gain_sb[:, 1, t : t + 1])
-            late_bf[1, u] = work.tile([P, QUARTER * PACK], BF16, name="late_bf", tag="late_bf", bufs=4, align_bytes=64)
-            nc.scalar.copy(*woven(late_bf[1, u][:], planes[:]))
+            tiles = scale_tiles(th, 1)
+            nc.scalar.copy(*woven(quarter_bf(1, u)[:], tiles[:]))
 
         def quantize_quarter(g, u):
-            late_q[g, u] = held([P, QUARTER], U32, "late_q%d%d" % (g, u))
-            late_s[g, u] = held([P, QUARTER], U8, "late_s%d%d" % (g, u))
-            nc.vector.quantize_mx(out=late_q[g, u][:].bitcast(FP8X4), scales=late_s[g, u][:], in_=late_bf[g, u][:])
-
-        def finish_first_half(b, t):
-            acc = bank("c_ps")
-            pass_c(acc[:], 0, b, t, h_q[0, 0][:], h_s[0, 0][:], True, False)
-            pass_c(acc[:], 1, b, t, h_q[1, 0][:], h_s[1, 0][:], False, True)
-            res = result()
-            nc.vector.tensor_tensor(res[:], acc[:], a_sb[b, 0][:, t, :], ALU.add)
-            nc.sync.dma_start(out_rows(b)[:, t, 0:HALF], res[:])
-
-        opened = {}
+            late_q[g, u] = quantize(late_bf[g, u], QUARTER, "late%d%d" % (g, u))
 
         def open_residual(u):
             for pair in range(2):
@@ -338,9 +304,8 @@ def tile_list_merge_negotiation_costs_kernel(
                 for s in range(2):
                     for a in range(2):
                         for c in range(QUARTER // CHUNK):
-                            lo = c * CHUNK
-                            part = acc[:, s * QUARTER + lo : s * QUARTER + lo + CHUNK]
-                            js = slice(u * QUARTER + lo, u * QUARTER + lo + CHUNK)
+                            part = acc[:, span(s * (QUARTER // CHUNK) + c, CHUNK)]
+                            js = span(u * (QUARTER // CHUNK) + c, CHUNK)
                             pass_a(part, a, 1, 2 * pair + s, 1, js, (s, a, c) == (0, 0, 0), False)
 
         def open_costs(u):
@@ -349,88 +314,84 @@ def tile_list_merge_negotiation_costs_kernel(
                     if b == 0:
                         opened[u, pair, 0] = bank("c_ps")
                     for s in range(2):
-                        pass_c(
-                            opened[u, pair, b][:, span(s)], 0, b, 2 * pair + s, late_q[0, u][:], late_s[0, u][:],
-                            b == 0 and s == 0, False,
-                        )
+                        acc = opened[u, pair, b][:, span(s, QUARTER)]
+                        pass_cost(acc, 0, b, 2 * pair + s, *late_q[0, u], b == 0 and s == 0, False)
 
         def finish_quarter(u):
             for pair in range(2):
-                ts = slice(2 * pair, 2 * pair + 2)
-                for b in (1, 0):
+                ts = span(pair, 2)
+                for b in range(2):
                     acc = opened[u, pair, b]
                     for s in range(2):
-                        pass_c(acc[:, span(s)], 1, b, 2 * pair + s, late_q[1, u][:], late_s[1, u][:], False, s == 1)
+                        pass_cost(acc[:, span(s, QUARTER)], 1, b, 2 * pair + s, *late_q[1, u], False, s == 1)
                     res = result()
-                    two = res[:].rearrange("p (s j) -> p s j", s=2)
                     if b == 0:
-                        nc.vector.tensor_tensor(two, acc[:].rearrange("p (s j) -> p s j", s=2), a_sb[0, 1][:, ts, span(u)], ALU.add)
+                        nc.vector.tensor_tensor(pairs(res[:]), pairs(acc[:]), a_sb[0, 1][:, ts, span(u, QUARTER)], ALU.add)
                     else:
                         nc.scalar.copy(res[:], acc[:])
-                    nc.sync.dma_start(out_rows(b)[:, ts, HALF + u * QUARTER : HALF + (u + 1) * QUARTER], two)
+                    nc.sync.dma_start(out_rows(b)[:, ts, span(HALF // QUARTER + u, QUARTER)], pairs(res[:]))
 
-        grouped0, dst0, src0 = w2_views(0, w2_raw0)
-        w3_p = []
-
-        def reorder_w3():
-            for g in range(2):
-                w3_p.append(held([P, H], U32, "w3_p%d" % g))
-                nc.vector.tensor_copy(
-                    w3_p[g][:].rearrange("p (b t c i) -> p b c t i", t=PACK, i=4, b=2),
-                    w3_raw[:, g, :].bitcast(U32).rearrange("p (b c i t) -> p b c t i", t=PACK, i=4, b=2),
-                )
-
-        nc.scalar.activation(dst0, src0, ACT.Copy, scale=-1.0)
-        quantize_w2(0, grouped0)
         gather_v(0, 0, tab_w0)
         gather_v(0, 1, tab_w0)
-        w2_raw1 = load_w2(1, 9)
-        gain_sb = placed([P, 2, PACK], F32, "gain_sb", 17)
+        w2_raw1 = load_w2(1, 0)
+        gain_sb = placed([P, 2, PACK], F32, "gain_sb", 8)
         nc.sync.dma_start(gain_sb[:], gain.rearrange("(g p t) -> p g t", g=2, t=PACK))
         gather_v(1, 0, tab_w1)
         gather_v(1, 1, tab_w1)
-        w3_raw = placed([P, 2, H], I32, "w3_raw", 27)
+        w3_raw = placed([P, 2, H], I32, "w3_raw", 20)
         nc.sync.dma_start(w3_raw[:], w3_words.rearrange("a p c i -> p a (c i)").bitcast(I32))
+
         make_a(0, 0)
+        round_w2(0, w2_raw0)
         make_a(1, 0)
         gather_v2(0)
-        make_diff(0, 0)
-        gather_v2(1)
-        grouped1, dst1, src1 = w2_views(1, w2_raw1)
-        nc.vector.tensor_scalar(dst1, src1, -1.0, None, ALU.mult)
-        make_tanh(0, 0)
-        quantize_w2(1, grouped1)
+        quantize_w2(0)
         make_a(0, 1)
-        make_diff(1, 0)
-        reorder_w3()
-        make_h(0, 0)
-        make_tanh(1, 0)
-        quantize_h(0, 0)
+
+        diff_half(0)
+        gather_v2(1)
+        round_w2(1, w2_raw1)
+        th_half = [tanh_woven(diff[0][:, :, span(u, QUARTER)]) for u in range(2)]
+        quantize_w2(1)
+        diff_half(1)
+        reorder_w3(w3_raw)
+        half_bf(0)
+        for u in range(2):
+            weigh(h_bf[0][:, span(u, QUARTER * PACK)], th_half[u], 0)
+        tiles_half = held([P, PACK, HALF], BF16, "tiles_half")
+        for t in range(PACK):
+            th_tile = work.tile([P, HALF], F32, name="th_tile", tag="th_tile", bufs=4)
+            nc.scalar.activation(th_tile[:], diff[1][:, t, :], ACT.Tanh, bias=no_bias[:])
+            scale_tile(tiles_half[:, t, :], th_tile[:], 1, t)
+        quantize_half(0)
         diff_quarter(0)
-        make_h(1, 0)
-        tanh_quarter(0)
-        quantize_h(1, 0)
+        nc.vector.tensor_copy(*woven(half_bf(1)[:], tiles_half[:]))
+        th_first = tanh_woven(late_diff[0][:])
+        quantize_half(1)
+
         diff_quarter(1)
-        make_last(0)
-        tanh_quarter(1)
-        weigh_quarter(0)
-        finish_first_half(0, 0)
+        group1_quarter(0)
+        th_second = plain_tanh_tile()
+        nc.scalar.activation(th_second[:], late_diff[1][:], ACT.Tanh, bias=no_bias[:])
+        tiles_second = scale_tiles(th_second, 0)
+        weigh(quarter_bf(0, 0)[:], th_first, 0)
+        finish_half(0, 0)
         quantize_quarter(0, 0)
-        finish_first_half(0, 1)
+        finish_half(0, 1)
         quantize_quarter(1, 0)
-        make_last(1)
+        group1_quarter(1)
         open_residual(0)
-        finish_first_half(0, 2)
-        finish_first_half(0, 3)
+        finish_half(0, 2)
+        finish_half(0, 3)
         open_costs(0)
-        finish_first_half(1, 0)
+        finish_half(1, 0)
         finish_quarter(0)
-        finish_first_half(1, 1)
-        weigh_quarter(1)
-        finish_first_half(1, 2)
+        finish_half(1, 1)
+        nc.vector.tensor_copy(*woven(quarter_bf(0, 1)[:], tiles_second[:]))
+        finish_half(1, 2)
         open_residual(1)
         quantize_quarter(0, 1)
-        finish_first_half(1, 3)
+        finish_half(1, 3)
         open_costs(1)
         quantize_quarter(1, 1)
         finish_quarter(1)

from contextlib import ExitStack

import concourse.mybir as mybir

K, K2, H, T, S = 1024, 512, 1024, 4096, 1024
FLOPS = 2 * S * H * (K + K2 + H)

F32 = mybir.dt.float32
BF16 = mybir.dt.bfloat16
I32 = mybir.dt.int32
U32 = mybir.dt.uint32
U16 = mybir.dt.uint16
U8 = mybir.dt.uint8
FP8X4 = mybir.dt.float8_e4m3fn_x4
FP4X4 = mybir.dt.float4_e2m1fn_x4
ALU = mybir.AluOpType
ACT = mybir.ActivationFunctionType

P = 128
PACK = 4
GROUP = P * PACK
HALF = 512
QUARTER = 256
CHUNK = 128
QUAD = 32
ROWS = 4
RUN = 4


def tile_list_merge_negotiation_costs_kernel(
    tc, tab_words, tab_scales, tab2_words, tab2_scales, offs, offs2,
    w1_words, w1_scales, w2, gain, w3_words, w3_scales, out,
):
    nc = tc.nc
    with ExitStack() as ctx:
        lists = ctx.enter_context(tc.tile_pool(name="lists", bufs=1))
        keep = ctx.enter_context(tc.tile_pool(name="keep", bufs=1))
        shared = ctx.enter_context(tc.tile_pool(name="shared", bufs=1))
        work = ctx.enter_context(tc.tile_pool(name="work", bufs=2))
        psum = ctx.enter_context(tc.psum_pool(name="psum", bufs=8))

        def held(shape, dtype, name):
            return keep.tile(shape, dtype, name=name, tag=name, align_bytes=64)

        def placed(shape, dtype, name, kib):
            return shared.tile(shape, dtype, name=name, tag=name, align_bytes=64, offset=kib * 1024)

        def bank(name):
            return psum.tile([P, HALF], F32, name=name, tag="bank")

        def span(n, width):
            return slice(n * width, (n + 1) * width)

        idx = lists.tile([P, S // 16], U16, name="idx")
        idx2 = lists.tile([P, S // 16], U16, name="idx2")
        nc.sync.dma_start(idx[:], offs)
        nc.sync.dma_start(idx2[:], offs2)

        w1_raw = placed([P, 2, H // 2], I32, "w1_raw", 16)
        nc.sync.dma_start(w1_raw[:], w1_words.rearrange("a p c -> p a c").bitcast(I32))
        tab_s = placed([P, T // 4], I32, "tab_s", 35)
        v_planes = held([P, 2, S // 4], I32, "v_planes")
        v2_plane = held([P, S // 4], I32, "v2_plane")
        w_s = held([P, 2, H // 4], I32, "w_s")
        tab2_s = placed([P, T // 4], I32, "tab2_s", 45)
        zero = placed([P, 1], F32, "zero", 0)
        no_bias = held([P, 1], F32, "no_bias")
        nc.vector.memset(tab_s[:, 0 : T // 8], 0)
        nc.gpsimd.memset(tab_s[:, T // 8 : T // 4], 0)
        nc.vector.memset(zero[:], 0.0)
        nc.vector.memset(tab2_s[:], 0)
        nc.vector.memset(w_s[:], 0)
        nc.vector.memset(v_planes[:], 0)
        nc.vector.memset(v2_plane[:], 0)
        nc.scalar.activation(no_bias[:], zero[:], ACT.Tanh)

        tab_step, tab2_step, tab2_first = P // 32, P // 16, ROWS
        nc.sync.dma_start(tab_s[0:P:tab_step, :], tab_scales.rearrange("a q t -> (a q) t").bitcast(I32))
        nc.sync.dma_start(tab2_s[tab2_first:P:tab2_step, :], tab2_scales[0].bitcast(I32))
        for first, scales in ((0, w1_scales), (ROWS, w3_scales)):
            for q in range(P // QUAD):
                nc.sync.dma_start(
                    w_s[QUAD * q + first : QUAD * q + first + ROWS, :, :],
                    scales[:, span(q, ROWS), :].rearrange("a r c -> r a c").bitcast(I32),
                )

        def load_table_pass(a, kib):
            words = placed([P, T], I32, "tab_w%d" % a, kib)
            nc.sync.dma_start(words[:], tab_words[a].rearrange("p t i -> p (t i)").bitcast(I32))
            return words

        def load_w2(g, kib):
            raw = placed([P, PACK, GROUP], F32, "w2_raw%d" % g, kib)
            nc.sync.dma_start(raw[:], w2[:, span(g, GROUP)].rearrange("(p j) c -> p j c", j=PACK))
            return raw

        def reorder_columns(dst, src):
            nc.vector.tensor_copy(
                dst.rearrange("p (g t m) -> p g t m", t=PACK, m=P),
                src.rearrange("p (g m t) -> p g t m", t=PACK, m=P),
            )

        def move_rows(plane, gathered, first, step):
            for q in range(P // QUAD):
                lo = first + step * ROWS * q
                nc.sync.dma_start(
                    plane[QUAD * q : QUAD * q + ROWS, :],
                    gathered[lo : lo + step * (ROWS - 1) + 1 : step, :].bitcast(I32),
                )

        tab_w0 = load_table_pass(0, 0)
        w1_p = held([P, 2 * H], U16, "w1_p")
        reorder_columns(w1_p[:], w1_raw[:].rearrange("p a c -> p (a c)").bitcast(U16))

        v_rows = placed([P, S], U8, "v_rows", 16)
        nc.vector.tensor_copy(v_rows[:], tab_s[:].bitcast(U8).indirect(idx[:]))
        move_rows(v_planes[:, 0, :], v_rows, 0, tab_step)
        tab_w1 = load_table_pass(1, 20)
        move_rows(v_planes[:, 1, :], v_rows, 16 * tab_step, tab_step)

        v2_rows = placed([P, S], U8, "v2_rows", 36)
        nc.vector.tensor_copy(v2_rows[:], tab2_s[:].bitcast(U8).indirect(idx2[:]))
        w2_raw0 = load_w2(0, 39)
        tab2_w = placed([P, T // 2], I32, "tab2_w", 47)
        nc.sync.dma_start(tab2_w[:], tab2_words[0].bitcast(I32))
        move_rows(v2_plane, v2_rows, tab2_first, tab2_step)

        w_planes = placed([P, 2 * H], U8, "w_planes", 37)
        reorder_columns(w_planes[:], w_s[:].rearrange("p a c -> p (a c)").bitcast(U8))

        v, v2 = {}, {}

        def gather_v(a, h, window):
            v[a, h] = held([P, HALF], U32, "v%d%d" % (a, h))
            nc.vector.tensor_copy(v[a, h][:], window[:].bitcast(U32).indirect(idx[:, span(h, HALF // 16)]))

        def gather_v2(h):
            v2[h] = held([P, HALF], U16, "v2%d" % h)
            nc.vector.tensor_copy(v2[h][:], tab2_w[:].bitcast(U16).indirect(idx2[:, span(h, HALF // 16)]))

        w2_bf, w2_q, w2_s = {}, {}, {}

        def round_w2(g, raw):
            w2_bf[g] = held([P, PACK * GROUP], BF16, "w2_bf%d" % g)
            nc.vector.tensor_scalar(
                w2_bf[g][:].rearrange("p (t m j) -> p m j t", t=PACK, j=PACK),
                raw[:].rearrange("p j (m t) -> p m j t", t=PACK),
                -1.0, None, ALU.mult,
            )

        def quantize(values, width, name):
            words = held([P, width], U32, name + "_q")
            plane = held([P, width], U8, name + "_s")
            nc.vector.quantize_mx(out=words[:].bitcast(FP8X4), scales=plane[:], in_=values[:])
            return words, plane

        def quantize_w2(g):
            w2_q[g], w2_s[g] = quantize(w2_bf[g], GROUP, "w2_%d" % g)

        w3_p = []

        def reorder_w3(raw):
            for g in range(2):
                w3_p.append(held([P, H], U32, "w3_p%d" % g))
                nc.vector.tensor_copy(
                    w3_p[g][:].rearrange("p (b t c i) -> p b c t i", t=PACK, i=RUN, b=2),
                    raw[:, g, :].bitcast(U32).rearrange("p (b c i t) -> p b c t i", t=PACK, i=RUN, b=2),
                )

        def pass_a(acc, a, g, t, h, js, start, stop):
            cols = span((a * H + g * GROUP) // P + t, P)
            entries = slice(h * HALF + js.start, h * HALF + js.stop)
            nc.tensor.matmul_mx(
                out=acc, lhsT=w1_p[:, cols].bitcast(FP4X4), lhsT_scale=w_planes[:, cols],
                rhs=v[a, h][:, js].bitcast(FP8X4), rhs_scale=v_planes[:, a, :].bitcast(U8)[:, entries],
                start=start, stop=stop,
            )

        def pass_b(acc, g, t, h, js, start, stop):
            entries = slice(h * HALF + js.start, h * HALF + js.stop)
            nc.tensor.matmul_mx(
                out=acc, lhsT=w2_q[g][:, span(t, P)].bitcast(FP8X4), lhsT_scale=w2_s[g][:, span(t, P)],
                rhs=v2[h][:, js].bitcast(FP4X4), rhs_scale=v2_plane[:].bitcast(U8)[:, entries],
                start=start, stop=stop,
            )

        def pass_cost(acc, g, b, t, h_words, h_plane, start, stop):
            nc.tensor.matmul_mx(
                out=acc, lhsT=w3_p[g][:, span(b * PACK + t, P)].bitcast(FP8X4),
                lhsT_scale=w_planes[ROWS:P, span((g * H + b * GROUP) // P + t, P)],
                rhs=h_words[:].bitcast(FP8X4), rhs_scale=h_plane[:], start=start, stop=stop,
            )

        def woven(dst, src):
            return (
                dst.rearrange("p (c i t) -> p c t i", i=RUN, t=PACK),
                src.rearrange("p t (c i) -> p c t i", i=RUN),
            )

        def pairs(acc):
            return acc.rearrange("p (s j) -> p s j", s=2)

        whole = span(0, HALF)
        a_sb, diff, h_bf, h_q = {}, {}, {}, {}

        def make_a(g, h):
            a_sb[g, h] = held([P, PACK, HALF], F32, "a%d%d" % (g, h))
            for t in range(PACK):
                acc = bank("a_ps")
                pass_a(acc[:], 0, g, t, h, whole, True, False)
                pass_a(acc[:], 1, g, t, h, whole, False, True)
                nc.scalar.copy(a_sb[g, h][:, t, :], acc[:])

        def tanh_woven(src):
            th = work.tile([P, QUARTER * PACK], F32, name="th", tag="th", bufs=3)
            dst, tiles = woven(th[:], src)
            nc.scalar.activation(dst, tiles, ACT.Tanh, bias=no_bias[:])
            return th

        def weigh(dst, th, g):
            nc.vector.tensor_tensor(
                dst.rearrange("p (j t) -> p j t", t=PACK), th[:].rearrange("p (j t) -> p j t", t=PACK),
                gain_sb[:, g : g + 1, :].to_broadcast([P, QUARTER, PACK]), ALU.mult,
            )

        def scale_tile(dst, th, g, t):
            nc.scalar.activation(dst, th, ACT.Copy, scale=gain_sb[:, g, t : t + 1])

        def scale_tiles(th, g):
            tiles = work.tile([P, PACK, QUARTER], BF16, name="tiles", tag="tiles", bufs=4)
            for t in range(PACK):
                scale_tile(tiles[:, t, :], th[:, t, :], g, t)
            return tiles

        def out_rows(b):
            return out[span(b, GROUP), :].rearrange("(p t) j -> p t j", t=PACK)

        def result():
            return work.tile([P, HALF], F32, name="res", tag="res", bufs=8)

        def diff_half(g):
            diff[g] = work.tile([P, PACK, HALF], F32, name="diff", tag="diff")
            for t in range(PACK):
                acc = bank("b_ps")
                pass_b(acc[:], g, t, 0, whole, True, True)
                nc.vector.tensor_tensor(diff[g][:, t, :], acc[:], a_sb[g, 0][:, t, :], ALU.add)

        def half_bf(g):
            h_bf[g] = work.tile([P, HALF * PACK], BF16, name="h_bf", tag="h_bf", align_bytes=64)
            return h_bf[g]

        def quantize_half(g):
            h_q[g] = quantize(h_bf[g], HALF, "h%d" % g)

        def finish_half(b, t):
            acc = bank("c_ps")
            pass_cost(acc[:], 0, b, t, *h_q[0], True, False)
            pass_cost(acc[:], 1, b, t, *h_q[1], False, True)
            res = result()
            nc.vector.tensor_tensor(res[:], acc[:], a_sb[b, 0][:, t, :], ALU.add)
            nc.sync.dma_start(out_rows(b)[:, t, 0:HALF], res[:])

        late_diff, late_bf, late_q, opened = {}, {}, {}, {}

        def diff_quarter(u):
            late_diff[u] = work.tile([P, PACK, QUARTER], F32, name="late_diff", tag="late_diff")
            for pair in range(2):
                acc = bank("b_ps")
                for s in range(2):
                    pass_b(acc[:, span(s, QUARTER)], 0, 2 * pair + s, 1, span(u, QUARTER), True, True)
                ts = span(pair, 2)
                nc.vector.tensor_tensor(late_diff[u][:, ts, :], pairs(acc[:]), a_sb[0, 1][:, ts, span(u, QUARTER)], ALU.add)

        def quarter_bf(g, u):
            late_bf[g, u] = work.tile([P, QUARTER * PACK], BF16, name="late_bf", tag="late_bf", bufs=4, align_bytes=64)
            return late_bf[g, u]

        def plain_tanh_tile():
            return work.tile([P, PACK, QUARTER], F32, name="th_plain", tag="th_plain", bufs=3)

        def group1_quarter(u):
            th = plain_tanh_tile()
            for c in range(QUARTER // CHUNK):
                js = span(u * (QUARTER // CHUNK) + c, CHUNK)
                acc = bank("d_ps")
                for t in range(PACK):
                    part = acc[:, span(t, CHUNK)]
                    pass_a(part, 0, 1, t, 1, js, True, False)
                    pass_a(part, 1, 1, t, 1, js, False, False)
                    pass_b(part, 1, t, 1, js, False, True)
                nc.scalar.activation(
                    th[:, :, span(c, CHUNK)], acc[:].rearrange("p (t j) -> p t j", t=PACK), ACT.Tanh, bias=no_bias[:]
                )
            tiles = scale_tiles(th, 1)
            nc.scalar.copy(*woven(quarter_bf(1, u)[:], tiles[:]))

        def quantize_quarter(g, u):
            late_q[g, u] = quantize(late_bf[g, u], QUARTER, "late%d%d" % (g, u))

        def open_residual(u):
            for pair in range(2):
                acc = bank("c_ps")
                opened[u, pair, 1] = acc
                for s in range(2):
                    for a in range(2):
                        for c in range(QUARTER // CHUNK):
                            part = acc[:, span(s * (QUARTER // CHUNK) + c, CHUNK)]
                            js = span(u * (QUARTER // CHUNK) + c, CHUNK)
                            pass_a(part, a, 1, 2 * pair + s, 1, js, (s, a, c) == (0, 0, 0), False)

        def open_costs(u):
            for pair in range(2):
                for b in (1, 0):
                    if b == 0:
                        opened[u, pair, 0] = bank("c_ps")
                    for s in range(2):
                        acc = opened[u, pair, b][:, span(s, QUARTER)]
                        pass_cost(acc, 0, b, 2 * pair + s, *late_q[0, u], b == 0 and s == 0, False)

        def finish_quarter(u):
            for pair in range(2):
                ts = span(pair, 2)
                for b in range(2):
                    acc = opened[u, pair, b]
                    for s in range(2):
                        pass_cost(acc[:, span(s, QUARTER)], 1, b, 2 * pair + s, *late_q[1, u], False, s == 1)
                    res = result()
                    if b == 0:
                        nc.vector.tensor_tensor(pairs(res[:]), pairs(acc[:]), a_sb[0, 1][:, ts, span(u, QUARTER)], ALU.add)
                    else:
                        nc.scalar.copy(res[:], acc[:])
                    nc.sync.dma_start(out_rows(b)[:, ts, span(HALF // QUARTER + u, QUARTER)], pairs(res[:]))

        gather_v(0, 0, tab_w0)
        gather_v(0, 1, tab_w0)
        w2_raw1 = load_w2(1, 0)
        gain_sb = placed([P, 2, PACK], F32, "gain_sb", 8)
        nc.sync.dma_start(gain_sb[:], gain.rearrange("(g p t) -> p g t", g=2, t=PACK))
        gather_v(1, 0, tab_w1)
        gather_v(1, 1, tab_w1)
        w3_raw = placed([P, 2, H], I32, "w3_raw", 20)
        nc.sync.dma_start(w3_raw[:], w3_words.rearrange("a p c i -> p a (c i)").bitcast(I32))

        make_a(0, 0)
        round_w2(0, w2_raw0)
        make_a(1, 0)
        gather_v2(0)
        quantize_w2(0)
        make_a(0, 1)

        diff_half(0)
        gather_v2(1)
        round_w2(1, w2_raw1)
        th_half = [tanh_woven(diff[0][:, :, span(u, QUARTER)]) for u in range(2)]
        quantize_w2(1)
        diff_half(1)
        reorder_w3(w3_raw)
        half_bf(0)
        for u in range(2):
            weigh(h_bf[0][:, span(u, QUARTER * PACK)], th_half[u], 0)
        tiles_half = held([P, PACK, HALF], BF16, "tiles_half")
        for t in range(PACK):
            th_tile = work.tile([P, HALF], F32, name="th_tile", tag="th_tile", bufs=4)
            nc.scalar.activation(th_tile[:], diff[1][:, t, :], ACT.Tanh, bias=no_bias[:])
            scale_tile(tiles_half[:, t, :], th_tile[:], 1, t)
        quantize_half(0)
        diff_quarter(0)
        nc.vector.tensor_copy(*woven(half_bf(1)[:], tiles_half[:]))
        th_first = tanh_woven(late_diff[0][:])
        quantize_half(1)

        diff_quarter(1)
        group1_quarter(0)
        th_second = plain_tanh_tile()
        nc.scalar.activation(th_second[:], late_diff[1][:], ACT.Tanh, bias=no_bias[:])
        tiles_second = scale_tiles(th_second, 0)
        weigh(quarter_bf(0, 0)[:], th_first, 0)
        finish_half(0, 0)
        quantize_quarter(0, 0)
        finish_half(0, 1)
        quantize_quarter(1, 0)
        group1_quarter(1)
        open_residual(0)
        finish_half(0, 2)
        finish_half(0, 3)
        open_costs(0)
        finish_half(1, 0)
        finish_quarter(0)
        finish_half(1, 1)
        nc.vector.tensor_copy(*woven(quarter_bf(0, 1)[:], tiles_second[:]))
        finish_half(1, 2)
        open_residual(1)
        quantize_quarter(0, 1)
        finish_half(1, 3)
        open_costs(1)
        quantize_quarter(1, 1)
        finish_quarter(1)
